import numpy as np
import ml_dtypes


def mxq(x, axis, fmt="e4m3"):
    dtype, down = {"e4m3": (ml_dtypes.float8_e4m3fn, 7), "e5m2": (ml_dtypes.float8_e5m2, 14)}[fmt]
    v = np.moveaxis(np.asarray(x, np.float32).astype(ml_dtypes.bfloat16).astype(np.float64), axis, -1)
    blocks = v.reshape(v.shape[:-1] + (-1, 32))
    amax = np.abs(blocks).max(-1, keepdims=True)
    byte = np.maximum(np.where(amax > 0, np.frexp(amax)[1] - 1 + 127, 0) - down, 1)
    scale = np.exp2(byte - 127.0)
    codes = (blocks / scale).astype(np.float32).astype(dtype).astype(np.float64)
    return np.moveaxis((codes * scale).reshape(v.shape), -1, axis)


WIDE = False


def mx_kscale(k):
    if not WIDE:
        return np.ones(k)
    levels = np.array([10, -10, 5, -5, 0])
    if k % 512:
        return np.exp2(np.random.permutation(np.resize(levels, k // 32))).repeat(32)
    a = np.empty((k // 512, 16))
    for p in range(k // 512):
        a[p, :8] = np.random.permutation(np.resize(levels, 8))
        for g in range(8):
            far = levels[np.abs(levels - a[p, g]) >= 10]
            a[p, g + 8] = far[np.random.randint(len(far))]
    return np.exp2(a.ravel()).repeat(32)


def f64(x):
    return np.asarray(x).astype(np.float64)


def striped(idx):
    return np.tile(idx.reshape(-1, 16).T, (8, 1)).astype(np.uint16)


def unstriped(offs):
    return offs[:16].T.reshape(-1).astype(np.int64)


E2M1 = np.array([0.0, 0.5, 1.0, 1.5, 2.0, 3.0, 4.0, 6.0, -0.0, -0.5, -1.0, -1.5, -2.0, -3.0, -4.0, -6.0])


def pack_weight(w, fmt):
    k, n = w.shape
    w = f64(np.asarray(w, np.float32).astype(ml_dtypes.bfloat16)).reshape(k // 32, 32, n)
    amax = np.abs(w).max(1)
    if fmt == "e4m3":
        byte = np.frexp(amax)[1] - 1 + 127 - 7
    else:
        mant, ex = np.frexp(amax / 6.0)
        byte = np.where(mant > 0.5, ex, ex - 1) + 127
    byte = np.clip(np.where(amax > 0, byte, 1), 1, 254)
    scaled = (w * np.exp2(127.0 - byte)[:, None, :]).reshape(k, n).astype(np.float32)
    by_word = np.ascontiguousarray(scaled.reshape(k // 512, 128, 4, n).transpose(0, 1, 3, 2))
    if fmt == "e4m3":
        words = by_word.astype(ml_dtypes.float8_e4m3fn).view(np.uint8)
    else:
        c = by_word.astype(ml_dtypes.float4_e2m1fn).view(np.uint8) & 0xF
        words = (c[..., 0::2] | (c[..., 1::2] << 4)).reshape(k // 512, 128, 2 * n)
    return np.ascontiguousarray(words), np.ascontiguousarray(byte.astype(np.uint8).reshape(k // 512, 16, n))


def unpack_weight(words, scales, fmt):
    g, _, n = scales.shape
    words = np.ascontiguousarray(words).reshape(g, 128, n, -1)
    if fmt == "e4m3":
        vals = words.view(ml_dtypes.float8_e4m3fn).astype(np.float64)
    else:
        nib = np.empty((g, 128, n, 4), np.uint8)
        nib[..., 0::2] = words & 0xF
        nib[..., 1::2] = words >> 4
        vals = E2M1[nib]
    vals = vals * np.repeat(np.exp2(scales.astype(np.float64) - 127.0), 8, axis=1)[..., None]
    return vals.transpose(0, 1, 3, 2).reshape(g * 512, n)


def gelu(v):
    return 0.5 * v * (1.0 + np.tanh(np.sqrt(2.0 / np.pi) * (v + 0.044715 * v**3)))


K, H, N, T, S, T2 = 1024, 1536, 512, 4096, 1024, 2048

def setup_inputs():
    n = np.random.standard_normal
    s = mx_kscale(K)[:, None]
    u = mx_kscale(H)[:, None]
    tab_words, tab_scales = pack_weight(n((K, T)) * s, "e4m3")
    w2_words, w2_scales = pack_weight(n((H, N)) / np.sqrt(H) / u, "e2m1")
    return {
        "tab_words": tab_words, "tab_scales": tab_scales,
        "offs": striped(np.random.permutation(T)[:S]),
        "w1": (n((K, H)) / np.sqrt(K) / s).astype(np.float32),
        "gain": (np.exp(0.3 * n(H)) * u[:, 0]).astype(np.float32),
        "w2_words": w2_words, "w2_scales": w2_scales,
        "b2": (0.5 * n(N)).astype(np.float32),
        "wgo": np.exp(0.3 * n((128, S))).astype(np.float32),
        "offs2": striped(np.random.permutation(T2)[:S]),
    }

def reference(tab_words, tab_scales, offs, w1, gain, w2_words, w2_scales, b2, wgo, offs2):
    v = unpack_weight(tab_words, tab_scales, "e4m3")[:, unstriped(offs)]
    w1q = mxq(f64(w1), 0, "e4m3")
    a = w1q.T @ v
    h = f64(gain)[:, None] * np.square(np.maximum(a, 0.0))
    hq = mxq(h, 0, "e4m3")
    w2 = unpack_weight(w2_words, w2_scales, "e2m1")
    y = (w2.T @ hq) + f64(b2)[:, None]
    out = np.zeros((N, T2))
    out[:, unstriped(offs2)] = np.tile(f64(wgo), (N // 128, 1)) * y
    return out

@@ -1,0 +1,214 @@
+from contextlib import ExitStack
+
+import concourse.mybir as mybir
+
+K, H, N, T, S, T2 = 1024, 1536, 512, 4096, 1024, 2048
+FLOPS = 2 * K * H * S + 2 * H * N * S
+
+F32 = mybir.dt.float32
+BF16 = mybir.dt.bfloat16
+I32 = mybir.dt.int32
+U32 = mybir.dt.uint32
+U16 = mybir.dt.uint16
+U8 = mybir.dt.uint8
+FP8X4 = mybir.dt.float8_e4m3fn_x4
+FP4X4 = mybir.dt.float4_e2m1fn_x4
+ALU = mybir.AluOpType
+ACT = mybir.ActivationFunctionType
+
+P = 128
+PACK = 4
+KP = P * PACK
+A_PASSES = K // KP
+B_BLOCKS = H // KP
+N_TILES = N // P
+CH = 256
+CHUNKS = S // CH
+TINY = 1e-30
+
+UNIT_ORDER = [(0, 0), (1, 0), (0, 1), (1, 1), (0, 2), (1, 2), (2, 0), (2, 1), (2, 2), (3, 0), (3, 1), (3, 2)]
+VECTOR_RELU = [(0, 2), (1, 2), (2, 0)]
+
+
+def tile_list_paged_relu2_compact_kernel(
+    tc, tab_words, tab_scales, offs, w1, gain, w2_words, w2_scales, b2, wgo, offs2, out
+):
+    nc = tc.nc
+    with ExitStack() as ctx:
+        keep = ctx.enter_context(tc.tile_pool(name="keep", bufs=1))
+        ring = ctx.enter_context(tc.tile_pool(name="ring", bufs=3))
+        ypool = ctx.enter_context(tc.tile_pool(name="ypool", bufs=8))
+        psum_a = ctx.enter_context(tc.psum_pool(name="psum_a", bufs=5))
+        psum_y = ctx.enter_context(tc.psum_pool(name="psum_y", bufs=3))
+
+        offs_sb = keep.tile([P, S // 16], U16, name="offs_sb")
+        nc.sync.dma_start(offs_sb[:], offs)
+        gain_sb = keep.tile([P, B_BLOCKS, PACK], F32, name="gain_sb")
+        nc.sync.dma_start(gain_sb[:], gain.rearrange("(b p t) -> p b t", p=P, t=PACK))
+
+        tsc = keep.tile([P, T // 4], I32, name="tsc", align_bytes=64)
+        nc.vector.memset(tsc[:], 0)
+        tsc_hbm = tab_scales.bitcast(I32)
+        for q in range(4):
+            nc.scalar.dma_start(tsc[32 * q : 32 * q + 8, :], tsc_hbm[:, 4 * q : 4 * q + 4, :])
+
+        tabw = []
+        for a in range(A_PASSES):
+            tw = keep.tile([P, T], I32, name="tabw%d" % a, align_bytes=64)
+            nc.sync.dma_start(tw[:], tab_words[a].rearrange("p t i -> p (t i)").bitcast(I32))
+            tabw.append(tw)
+
+        raw = {}
+        for b in range(B_BLOCKS):
+            for a in range(A_PASSES):
+                rw = keep.tile([P, PACK, KP], F32, name="raw%d%d" % (b, a), align_bytes=64)
+                nc.sync.dma_start(
+                    rw[:],
+                    w1[KP * a : KP * (a + 1), KP * b : KP * (b + 1)].rearrange("(p j) c -> p j c", j=PACK),
+                )
+                raw[b, a] = rw
+
+        w2w = keep.tile([P, B_BLOCKS, 2 * N], U8, name="w2w", align_bytes=64)
+        nc.sync.dma_start(w2w[:].bitcast(I32), w2_words.bitcast(I32).rearrange("b p c -> p b c"))
+        w2s = keep.tile([P, B_BLOCKS, N], U8, name="w2s", align_bytes=64)
+        nc.vector.memset(w2s[:].bitcast(I32), 0)
+        w2s_hbm = w2_scales.bitcast(I32).rearrange("b q c -> q b c")
+        for q in range(4):
+            nc.sync.dma_start(w2s[32 * q : 32 * q + 4].bitcast(I32), w2s_hbm[4 * q : 4 * q + 4])
+        b2_sb = keep.tile([P, N_TILES], F32, name="b2_sb")
+        with nc.allow_non_contiguous_dma(reason="one bias a partition"):
+            nc.sync.dma_start(b2_sb[:], b2.rearrange("(c p) -> p c", p=P))
+        offs2_sb = keep.tile([P, S // 16], U16, name="offs2_sb")
+        nc.sync.dma_start(offs2_sb[:], offs2)
+        wgo_sb = keep.tile([P, S], F32, name="wgo_sb")
+        nc.sync.dma_start(wgo_sb[:], wgo)
+
+        g = gain_sb[:].rearrange("p b t -> p (b t)")
+        width = B_BLOCKS * PACK
+        mag = keep.tile([P, width], F32, name="mag")
+        nc.vector.scalar_tensor_tensor(mag[:], g, -1.0, g, ALU.mult, ALU.max)
+        magc = keep.tile([P, width], F32, name="magc")
+        nc.vector.tensor_scalar(magc[:], mag[:], TINY, None, ALU.max)
+        root0 = keep.tile([P, width], F32, name="root0")
+        nc.scalar.activation(root0[:], magc[:], ACT.Sqrt)
+        pos = keep.tile([P, width], F32, name="pos")
+        nc.vector.tensor_scalar(pos[:], g, 0.0, None, ALU.is_gt)
+        neg = keep.tile([P, width], F32, name="neg")
+        nc.vector.tensor_scalar(neg[:], g, 0.0, None, ALU.is_lt)
+        sgn = keep.tile([P, B_BLOCKS, PACK], F32, name="sgn")
+        nc.vector.tensor_tensor(sgn[:].rearrange("p b t -> p (b t)"), pos[:], neg[:], ALU.subtract)
+        rec = keep.tile([P, width], F32, name="rec")
+        nc.vector.reciprocal(rec[:], root0[:])
+        quot = keep.tile([P, width], F32, name="quot")
+        nc.vector.tensor_tensor(quot[:], magc[:], rec[:], ALU.mult)
+        both = keep.tile([P, width], F32, name="both")
+        nc.vector.tensor_tensor(both[:], quot[:], root0[:], ALU.add)
+        root = keep.tile([P, width], F32, name="root")
+        nc.vector.tensor_scalar(root[:], both[:], 0.5, None, ALU.mult)
+        signs = keep.tile([P, B_BLOCKS, CH, PACK], BF16, name="signs", align_bytes=64)
+        for b in range(B_BLOCKS):
+            nc.vector.tensor_copy(signs[:, b], sgn[:, b : b + 1, :].to_broadcast([P, CH, PACK]))
+
+        vs = keep.tile([P, S], U8, name="vs", align_bytes=64)
+        nc.vector.tensor_copy(vs[:], tsc[:].bitcast(U8).indirect(offs_sb[:]))
+        vw = []
+        for a in range(A_PASSES):
+            gw = keep.tile([P, S], U32, name="vw%d" % a, align_bytes=64)
+            nc.vector.tensor_copy(gw[:], tabw[a][:].bitcast(U32).indirect(offs_sb[:]))
+            vw.append(gw)
+
+        slots = []
+        for n in range(N_TILES):
+            sl = keep.tile([P, T2], F32, name="slots%d" % n)
+            nc.gpsimd.memset(sl[:], 0.0)
+            slots.append(sl)
+
+        w1c, w1s = {}, {}
+        for b in range(B_BLOCKS):
+            for a in range(A_PASSES):
+                wb = ring.tile([P, PACK * KP], BF16, name="wb", align_bytes=64)
+                nc.vector.tensor_copy(
+                    wb[:].rearrange("p (t m j) -> p m j t", t=PACK, j=PACK),
+                    raw[b, a][:].rearrange("p j (m t) -> p m j t", t=PACK),
+                )
+                wc = keep.tile([P, KP], U32, name="w1c%d%d" % (b, a), align_bytes=64)
+                ws = keep.tile([P, KP], U8, name="w1s%d%d" % (b, a), align_bytes=64)
+                nc.vector.quantize_mx(out=wc[:].bitcast(FP8X4), scales=ws[:], in_=wb[:])
+                w1c[b, a], w1s[b, a] = wc, ws
+
+        hc, hs, ysb = {}, {}, {}
+
+        def hidden(c, b):
+            cols = slice(CH * c, CH * (c + 1))
+            r = ring.tile([P, PACK, CH], F32, name="r")
+            for half in range(2):
+                acc = psum_a.tile([P, 2, CH], F32, name="acc")
+                for u in range(2):
+                    t = 2 * half + u
+                    m = slice(P * t, P * (t + 1))
+                    for a in range(A_PASSES):
+                        nc.tensor.matmul_mx(
+                            out=acc[:, u, :],
+                            lhsT=w1c[b, a][:, m].bitcast(FP8X4),
+                            lhsT_scale=w1s[b, a][:, m],
+                            rhs=vw[a][:, cols].bitcast(FP8X4),
+                            rhs_scale=vs[4 * a :, cols],
+                            start=(a == 0),
+                            stop=(a == A_PASSES - 1),
+                        )
+                for u in range(2):
+                    t = 2 * half + u
+                    s = root[:, PACK * b + t : PACK * b + t + 1]
+                    if half == 1 and (c, b) in VECTOR_RELU:
+                        nc.vector.tensor_scalar(r[:, t, :], acc[:, u, :], 0.0, s, ALU.max, ALU.mult)
+                    else:
+                        nc.scalar.activation(r[:, t, :], acc[:, u, :], ACT.Relu, scale=s)
+            sq = ring.tile([P, CH * PACK], BF16, name="sq", align_bytes=64)
+            nc.scalar.activation(
+                sq[:].rearrange("p (c i t) -> p c t i", i=4, t=PACK),
+                r[:].rearrange("p t (c i) -> p c t i", i=4),
+                ACT.Square,
+            )
+            hb = ring.tile([P, CH * PACK], BF16, name="hb", align_bytes=64)
+            nc.vector.tensor_tensor(hb[:], sq[:], signs[:, b].rearrange("p c t -> p (c t)"), ALU.mult)
+            codes = keep.tile([P, CH], U32, name="hc%d%d" % (c, b), align_bytes=64)
+            scales = keep.tile([P, CH], U8, name="hs%d%d" % (c, b), align_bytes=64)
+            nc.vector.quantize_mx(out=codes[:].bitcast(FP8X4), scales=scales[:], in_=hb[:])
+            hc[c, b], hs[c, b] = codes, scales
+
+        def project(c):
+            for n in range(N_TILES):
+                acc = psum_y.tile([P, CH], F32, name="yacc")
+                for h in range(CH // P):
+                    cols = slice(P * h, P * (h + 1))
+                    for b in range(B_BLOCKS):
+                        nc.tensor.matmul_mx(
+                            out=acc[:, cols],
+                            lhsT=w2w[:, b, 2 * P * n : 2 * P * (n + 1)].bitcast(FP4X4),
+                            lhsT_scale=w2s[:, b, P * n : P * (n + 1)],
+                            rhs=hc[c, b][:, cols].bitcast(FP8X4),
+                            rhs_scale=hs[c, b][:, cols],
+                            start=(b == 0),
+                            stop=(b == B_BLOCKS - 1),
+                        )
+                y = ypool.tile([P, CH], F32, name="y")
+                nc.scalar.activation(y[:], acc[:], ACT.Identity, bias=b2_sb[:, n : n + 1])
+                ysb[c, n] = y
+
+        def scatter(c, n):
+            places = offs2_sb[:, CH // 16 * c : CH // 16 * (c + 1)]
+            nc.vector.tensor_tensor(
+                slots[n][:].indirect(places), ysb[c, n][:], wgo_sb[:, CH * c : CH * (c + 1)], ALU.mult
+            )
+
+        for c, b in UNIT_ORDER:
+            hidden(c, b)
+            if b == B_BLOCKS - 1:
+                project(c)
+                if c < CHUNKS - 2:
+                    for n in range(N_TILES):
+                        scatter(c, n)
+        for n in range(N_TILES):
+            for c in range(CHUNKS - 2, CHUNKS):
+                scatter(c, n)
+            nc.sync.dma_start(out[P * n : P * (n + 1), :], slots[n][:])

@@ -27,7 +27,8 @@ CHUNKS = S // CH
 TINY = 1e-30
 
 UNIT_ORDER = [(0, 0), (1, 0), (0, 1), (1, 1), (0, 2), (1, 2), (2, 0), (2, 1), (2, 2), (3, 0), (3, 1), (3, 2)]
-VECTOR_RELU = [(0, 2), (1, 2), (2, 0)]
+SCATTERS = [[(0, 1), (1, 2), (2, 3), (3, 4)]] * 2 + [[(0, 1), (1, 2), (2, 4)]] * 2
+VECTOR_RELU = [(0, 2), (1, 2)]
 
 
 def tile_list_paged_relu2_compact_kernel(
@@ -37,16 +38,15 @@ def tile_list_paged_relu2_compact_kernel(
     with ExitStack() as ctx:
         keep = ctx.enter_context(tc.tile_pool(name="keep", bufs=1))
         ring = ctx.enter_context(tc.tile_pool(name="ring", bufs=3))
-        ypool = ctx.enter_context(tc.tile_pool(name="ypool", bufs=8))
         psum_a = ctx.enter_context(tc.psum_pool(name="psum_a", bufs=5))
         psum_y = ctx.enter_context(tc.psum_pool(name="psum_y", bufs=3))
 
         offs_sb = keep.tile([P, S // 16], U16, name="offs_sb")
         nc.sync.dma_start(offs_sb[:], offs)
-        gain_sb = keep.tile([P, B_BLOCKS, PACK], F32, name="gain_sb")
+        gain_sb = keep.tile([P, B_BLOCKS, PACK], F32, name="gain_sb", tag="vector")
         nc.sync.dma_start(gain_sb[:], gain.rearrange("(b p t) -> p b t", p=P, t=PACK))
 
-        tsc = keep.tile([P, T // 4], I32, name="tsc", align_bytes=64)
+        tsc = keep.tile([P, T // 4], I32, name="tsc", tag="planes", align_bytes=64)
         nc.vector.memset(tsc[:], 0)
         tsc_hbm = tab_scales.bitcast(I32)
         for q in range(4):
@@ -54,34 +54,23 @@ def tile_list_paged_relu2_compact_kernel(
 
         tabw = []
         for a in range(A_PASSES):
-            tw = keep.tile([P, T], I32, name="tabw%d" % a, align_bytes=64)
+            tw = keep.tile([P, T], I32, name="tabw%d" % a, tag="big%d" % a, align_bytes=64)
             nc.sync.dma_start(tw[:], tab_words[a].rearrange("p t i -> p (t i)").bitcast(I32))
             tabw.append(tw)
 
         raw = {}
-        for b in range(B_BLOCKS):
-            for a in range(A_PASSES):
-                rw = keep.tile([P, PACK, KP], F32, name="raw%d%d" % (b, a), align_bytes=64)
-                nc.sync.dma_start(
-                    rw[:],
-                    w1[KP * a : KP * (a + 1), KP * b : KP * (b + 1)].rearrange("(p j) c -> p j c", j=PACK),
-                )
-                raw[b, a] = rw
 
-        w2w = keep.tile([P, B_BLOCKS, 2 * N], U8, name="w2w", align_bytes=64)
-        nc.sync.dma_start(w2w[:].bitcast(I32), w2_words.bitcast(I32).rearrange("b p c -> p b c"))
-        w2s = keep.tile([P, B_BLOCKS, N], U8, name="w2s", align_bytes=64)
-        nc.vector.memset(w2s[:].bitcast(I32), 0)
-        w2s_hbm = w2_scales.bitcast(I32).rearrange("b q c -> q b c")
-        for q in range(4):
-            nc.sync.dma_start(w2s[32 * q : 32 * q + 4].bitcast(I32), w2s_hbm[4 * q : 4 * q + 4])
-        b2_sb = keep.tile([P, N_TILES], F32, name="b2_sb")
-        with nc.allow_non_contiguous_dma(reason="one bias a partition"):
-            nc.sync.dma_start(b2_sb[:], b2.rearrange("(c p) -> p c", p=P))
+        def load_w1(b, a, dst):
+            nc.sync.dma_start(
+                dst, w1[KP * a : KP * (a + 1), KP * b : KP * (b + 1)].rearrange("(p j) c -> p j c", j=PACK)
+            )
+            raw[b, a] = dst
+
+        for a in range(A_PASSES):
+            rw = keep.tile([P, PACK, KP], F32, name="raw0%d" % a, tag="first%d" % a, align_bytes=64)
+            load_w1(0, a, rw[:])
         offs2_sb = keep.tile([P, S // 16], U16, name="offs2_sb")
         nc.sync.dma_start(offs2_sb[:], offs2)
-        wgo_sb = keep.tile([P, S], F32, name="wgo_sb")
-        nc.sync.dma_start(wgo_sb[:], wgo)
 
         g = gain_sb[:].rearrange("p b t -> p (b t)")
         width = B_BLOCKS * PACK
@@ -95,7 +84,7 @@ def tile_list_paged_relu2_compact_kernel(
         nc.vector.tensor_scalar(pos[:], g, 0.0, None, ALU.is_gt)
         neg = keep.tile([P, width], F32, name="neg")
         nc.vector.tensor_scalar(neg[:], g, 0.0, None, ALU.is_lt)
-        sgn = keep.tile([P, B_BLOCKS, PACK], F32, name="sgn")
+        sgn = keep.tile([P, B_BLOCKS, PACK], BF16, name="sgn")
         nc.vector.tensor_tensor(sgn[:].rearrange("p b t -> p (b t)"), pos[:], neg[:], ALU.subtract)
         rec = keep.tile([P, width], F32, name="rec")
         nc.vector.reciprocal(rec[:], root0[:])
@@ -105,9 +94,6 @@ def tile_list_paged_relu2_compact_kernel(
         nc.vector.tensor_tensor(both[:], quot[:], root0[:], ALU.add)
         root = keep.tile([P, width], F32, name="root")
         nc.vector.tensor_scalar(root[:], both[:], 0.5, None, ALU.mult)
-        signs = keep.tile([P, B_BLOCKS, CH, PACK], BF16, name="signs", align_bytes=64)
-        for b in range(B_BLOCKS):
-            nc.vector.tensor_copy(signs[:, b], sgn[:, b : b + 1, :].to_broadcast([P, CH, PACK]))
 
         vs = keep.tile([P, S], U8, name="vs", align_bytes=64)
         nc.vector.tensor_copy(vs[:], tsc[:].bitcast(U8).indirect(offs_sb[:]))
@@ -117,26 +103,45 @@ def tile_list_paged_relu2_compact_kernel(
             nc.vector.tensor_copy(gw[:], tabw[a][:].bitcast(U32).indirect(offs_sb[:]))
             vw.append(gw)
 
+        for b in range(1, B_BLOCKS):
+            rw = keep.tile([P, A_PASSES, PACK, KP], F32, name="raw%d" % b, tag="big%d" % (b - 1), align_bytes=64)
+            for a in range(A_PASSES):
+                load_w1(b, a, rw[:, a])
+        w2s = keep.tile([P, B_BLOCKS, N], U8, name="w2s", tag="planes", align_bytes=64)
+        nc.vector.memset(w2s[:].bitcast(I32), 0)
+        w2s_hbm = w2_scales.bitcast(I32).rearrange("b q c -> q b c")
+        for q in range(4):
+            nc.sync.dma_start(w2s[32 * q : 32 * q + 4].bitcast(I32), w2s_hbm[4 * q : 4 * q + 4])
+        b2_sb = keep.tile([P, N_TILES], F32, name="b2_sb", tag="vector")
+        with nc.allow_non_contiguous_dma(reason="one bias a partition"):
+            nc.sync.dma_start(b2_sb[:], b2.rearrange("(c p) -> p c", p=P))
+
         slots = []
         for n in range(N_TILES):
             sl = keep.tile([P, T2], F32, name="slots%d" % n)
-            nc.gpsimd.memset(sl[:], 0.0)
+            nc.vector.memset(sl[:], 0.0)
             slots.append(sl)
 
         w1c, w1s = {}, {}
         for b in range(B_BLOCKS):
             for a in range(A_PASSES):
-                wb = ring.tile([P, PACK * KP], BF16, name="wb", align_bytes=64)
+                wb = ring.tile([P, PACK * KP], BF16, name="wb", align_bytes=64, bufs=2)
                 nc.vector.tensor_copy(
                     wb[:].rearrange("p (t m j) -> p m j t", t=PACK, j=PACK),
-                    raw[b, a][:].rearrange("p j (m t) -> p m j t", t=PACK),
+                    raw[b, a].rearrange("p j (m t) -> p m j t", t=PACK),
                 )
                 wc = keep.tile([P, KP], U32, name="w1c%d%d" % (b, a), align_bytes=64)
                 ws = keep.tile([P, KP], U8, name="w1s%d%d" % (b, a), align_bytes=64)
                 nc.vector.quantize_mx(out=wc[:].bitcast(FP8X4), scales=ws[:], in_=wb[:])
                 w1c[b, a], w1s[b, a] = wc, ws
 
-        hc, hs, ysb = {}, {}, {}
+        w2w = keep.tile([P, B_BLOCKS, 2 * N], U8, name="w2w", tag="first0", align_bytes=64)
+        nc.sync.dma_start(w2w[:].bitcast(I32), w2_words.bitcast(I32).rearrange("b p c -> p b c"))
+        wgo_sb = keep.tile([P, S], F32, name="wgo_sb", tag="first1", align_bytes=64)
+        nc.sync.dma_start(wgo_sb[:], wgo)
+
+        hc, hs = {}, {}
+        ysb = [keep.tile([P, S], F32, name="y%d" % n) for n in range(N_TILES)]
 
         def hidden(c, b):
             cols = slice(CH * c, CH * (c + 1))
@@ -163,17 +168,21 @@ def tile_list_paged_relu2_compact_kernel(
                         nc.vector.tensor_scalar(r[:, t, :], acc[:, u, :], 0.0, s, ALU.max, ALU.mult)
                     else:
                         nc.scalar.activation(r[:, t, :], acc[:, u, :], ACT.Relu, scale=s)
-            sq = ring.tile([P, CH * PACK], BF16, name="sq", align_bytes=64)
+            sq = keep.tile([P, CH * PACK], BF16, name="sq%d%d" % (c, b), align_bytes=64)
             nc.scalar.activation(
                 sq[:].rearrange("p (c i t) -> p c t i", i=4, t=PACK),
                 r[:].rearrange("p t (c i) -> p c t i", i=4),
                 ACT.Square,
             )
-            hb = ring.tile([P, CH * PACK], BF16, name="hb", align_bytes=64)
-            nc.vector.tensor_tensor(hb[:], sq[:], signs[:, b].rearrange("p c t -> p (c t)"), ALU.mult)
+            nc.vector.tensor_tensor(
+                sq[:].rearrange("p (c t) -> p c t", t=PACK),
+                sq[:].rearrange("p (c t) -> p c t", t=PACK),
+                sgn[:, b : b + 1, :].to_broadcast([P, CH, PACK]),
+                ALU.mult,
+            )
             codes = keep.tile([P, CH], U32, name="hc%d%d" % (c, b), align_bytes=64)
             scales = keep.tile([P, CH], U8, name="hs%d%d" % (c, b), align_bytes=64)
-            nc.vector.quantize_mx(out=codes[:].bitcast(FP8X4), scales=scales[:], in_=hb[:])
+            nc.vector.quantize_mx(out=codes[:].bitcast(FP8X4), scales=scales[:], in_=sq[:])
             hc[c, b], hs[c, b] = codes, scales
 
         def project(c):
@@ -191,24 +200,20 @@ def tile_list_paged_relu2_compact_kernel(
                             start=(b == 0),
                             stop=(b == B_BLOCKS - 1),
                         )
-                y = ypool.tile([P, CH], F32, name="y")
-                nc.scalar.activation(y[:], acc[:], ACT.Identity, bias=b2_sb[:, n : n + 1])
-                ysb[c, n] = y
+                nc.scalar.activation(
+                    ysb[n][:, CH * c : CH * (c + 1)], acc[:], ACT.Identity, bias=b2_sb[:, n : n + 1]
+                )
 
-        def scatter(c, n):
-            places = offs2_sb[:, CH // 16 * c : CH // 16 * (c + 1)]
-            nc.vector.tensor_tensor(
-                slots[n][:].indirect(places), ysb[c, n][:], wgo_sb[:, CH * c : CH * (c + 1)], ALU.mult
-            )
+        def scatter(first, last, n):
+            places = offs2_sb[:, CH // 16 * first : CH // 16 * last]
+            cols = slice(CH * first, CH * last)
+            nc.vector.tensor_tensor(slots[n][:].indirect(places), ysb[n][:, cols], wgo_sb[:, cols], ALU.mult)
 
         for c, b in UNIT_ORDER:
             hidden(c, b)
             if b == B_BLOCKS - 1:
                 project(c)
-                if c < CHUNKS - 2:
-                    for n in range(N_TILES):
-                        scatter(c, n)
         for n in range(N_TILES):
-            for c in range(CHUNKS - 2, CHUNKS):
-                scatter(c, n)
+            for first, last in SCATTERS[n]:
+                scatter(first, last, n)
             nc.sync.dma_start(out[P * n : P * (n + 1), :], slots[n][:])

@@ -28,6 +28,7 @@ TINY = 1e-30
 
 UNIT_ORDER = [(0, 0), (1, 0), (0, 1), (1, 1), (0, 2), (1, 2), (2, 0), (2, 1), (2, 2), (3, 0), (3, 1), (3, 2)]
 SCATTERS = [[(0, 1), (1, 2), (2, 3), (3, 4)]] * 2 + [[(0, 1), (1, 2), (2, 4)]] * 2
+SCALAR_CASTS = [(0, 0)]
 VECTOR_RELU = [(0, 2), (1, 2)]
 
 
@@ -126,10 +127,13 @@ def tile_list_paged_relu2_compact_kernel(
         for b in range(B_BLOCKS):
             for a in range(A_PASSES):
                 wb = ring.tile([P, PACK * KP], BF16, name="wb", align_bytes=64, bufs=2)
-                nc.vector.tensor_copy(
-                    wb[:].rearrange("p (t m j) -> p m j t", t=PACK, j=PACK),
-                    raw[b, a].rearrange("p j (m t) -> p m j t", t=PACK),
-                )
+                dst = wb[:].rearrange("p (t m j) -> p m j t", t=PACK, j=PACK)
+                src = raw[b, a].rearrange("p j (m t) -> p m j t", t=PACK)
+                for t in range(0, PACK, 2):
+                    if (b, a) in SCALAR_CASTS:
+                        nc.scalar.copy(dst[:, :, :, t : t + 2], src[:, :, :, t : t + 2])
+                    else:
+                        nc.vector.tensor_copy(dst[:, :, :, t : t + 2], src[:, :, :, t : t + 2])
                 wc = keep.tile([P, KP], U32, name="w1c%d%d" % (b, a), align_bytes=64)
                 ws = keep.tile([P, KP], U8, name="w1s%d%d" % (b, a), align_bytes=64)
                 nc.vector.quantize_mx(out=wc[:].bitcast(FP8X4), scales=ws[:], in_=wb[:])

@@ -27,8 +27,14 @@ CHUNKS = S // CH
 TINY = 1e-30
 
 UNIT_ORDER = [(0, 0), (1, 0), (0, 1), (1, 1), (0, 2), (1, 2), (2, 0), (2, 1), (2, 2), (3, 0), (3, 1), (3, 2)]
-SCATTERS = [[(0, 1), (1, 2), (2, 3), (3, 4)]] * 2 + [[(0, 1), (1, 2), (2, 4)]] * 2
+SCATTERS = [[(0, 1), (1, 2), (2, 3), (3, 4)]] * 3 + [[(0, 1), (1, 2), (2, 4)]]
 SCALAR_CASTS = [(0, 0)]
+PROJECT_AFTER = {
+    (0, 2): [(0, [0, 1, 2, 3])],
+    (2, 1): [(1, [0, 1, 2, 3])],
+    (3, 1): [(2, [0, 1])],
+    (3, 2): [(2, [2, 3]), (3, [0, 1, 2, 3])],
+}
 VECTOR_RELU = [(0, 2), (1, 2)]
 
 
@@ -39,19 +45,21 @@ def tile_list_paged_relu2_compact_kernel(
     with ExitStack() as ctx:
         keep = ctx.enter_context(tc.tile_pool(name="keep", bufs=1))
         ring = ctx.enter_context(tc.tile_pool(name="ring", bufs=3))
-        psum_a = ctx.enter_context(tc.psum_pool(name="psum_a", bufs=5))
-        psum_y = ctx.enter_context(tc.psum_pool(name="psum_y", bufs=3))
+        psum_a = ctx.enter_context(tc.psum_pool(name="psum_a", bufs=6))
+        psum_y = ctx.enter_context(tc.psum_pool(name="psum_y", bufs=2))
 
         offs_sb = keep.tile([P, S // 16], U16, name="offs_sb")
         nc.sync.dma_start(offs_sb[:], offs)
         gain_sb = keep.tile([P, B_BLOCKS, PACK], F32, name="gain_sb", tag="vector")
         nc.sync.dma_start(gain_sb[:], gain.rearrange("(b p t) -> p b t", p=P, t=PACK))
 
+        offs2_sb = keep.tile([P, S // 16], U16, name="offs2_sb")
+        nc.sync.dma_start(offs2_sb[:], offs2)
         tsc = keep.tile([P, T // 4], I32, name="tsc", tag="planes", align_bytes=64)
         nc.vector.memset(tsc[:], 0)
         tsc_hbm = tab_scales.bitcast(I32)
         for q in range(4):
-            nc.scalar.dma_start(tsc[32 * q : 32 * q + 8, :], tsc_hbm[:, 4 * q : 4 * q + 4, :])
+            nc.sync.dma_start(tsc[32 * q : 32 * q + 8, :], tsc_hbm[:, 4 * q : 4 * q + 4, :])
 
         tabw = []
         for a in range(A_PASSES):
@@ -70,8 +78,6 @@ def tile_list_paged_relu2_compact_kernel(
         for a in range(A_PASSES):
             rw = keep.tile([P, PACK, KP], F32, name="raw0%d" % a, tag="first%d" % a, align_bytes=64)
             load_w1(0, a, rw[:])
-        offs2_sb = keep.tile([P, S // 16], U16, name="offs2_sb")
-        nc.sync.dma_start(offs2_sb[:], offs2)
 
         g = gain_sb[:].rearrange("p b t -> p (b t)")
         width = B_BLOCKS * PACK
@@ -96,6 +102,12 @@ def tile_list_paged_relu2_compact_kernel(
         root = keep.tile([P, width], F32, name="root")
         nc.vector.tensor_scalar(root[:], both[:], 0.5, None, ALU.mult)
 
+        slots = []
+        for n in range(N_TILES):
+            sl = keep.tile([P, T2], F32, name="slots%d" % n)
+            nc.vector.memset(sl[:], 0.0)
+            slots.append(sl)
+
         vs = keep.tile([P, S], U8, name="vs", align_bytes=64)
         nc.vector.tensor_copy(vs[:], tsc[:].bitcast(U8).indirect(offs_sb[:]))
         vw = []
@@ -116,12 +128,6 @@ def tile_list_paged_relu2_compact_kernel(
         b2_sb = keep.tile([P, N_TILES], F32, name="b2_sb", tag="vector")
         with nc.allow_non_contiguous_dma(reason="one bias a partition"):
             nc.sync.dma_start(b2_sb[:], b2.rearrange("(c p) -> p c", p=P))
-
-        slots = []
-        for n in range(N_TILES):
-            sl = keep.tile([P, T2], F32, name="slots%d" % n)
-            nc.vector.memset(sl[:], 0.0)
-            slots.append(sl)
 
         w1c, w1s = {}, {}
         for b in range(B_BLOCKS):
@@ -174,8 +180,8 @@ def tile_list_paged_relu2_compact_kernel(
                         nc.scalar.activation(r[:, t, :], acc[:, u, :], ACT.Relu, scale=s)
             sq = keep.tile([P, CH * PACK], BF16, name="sq%d%d" % (c, b), align_bytes=64)
             nc.scalar.activation(
-                sq[:].rearrange("p (c i t) -> p c t i", i=4, t=PACK),
-                r[:].rearrange("p t (c i) -> p c t i", i=4),
+                sq[:].rearrange("p (c t) -> p c t", t=PACK),
+                r[:].rearrange("p t c -> p c t"),
                 ACT.Square,
             )
             nc.vector.tensor_tensor(
@@ -189,8 +195,8 @@ def tile_list_paged_relu2_compact_kernel(
             nc.vector.quantize_mx(out=codes[:].bitcast(FP8X4), scales=scales[:], in_=sq[:])
             hc[c, b], hs[c, b] = codes, scales
 
-        def project(c):
-            for n in range(N_TILES):
+        def project(c, tiles):
+            for n in tiles:
                 acc = psum_y.tile([P, CH], F32, name="yacc")
                 for h in range(CH // P):
                     cols = slice(P * h, P * (h + 1))
@@ -215,8 +221,8 @@ def tile_list_paged_relu2_compact_kernel(
 
         for c, b in UNIT_ORDER:
             hidden(c, b)
-            if b == B_BLOCKS - 1:
-                project(c)
+            for chunk, tiles in PROJECT_AFTER.get((c, b), []):
+                project(chunk, tiles)
         for n in range(N_TILES):
             for first, last in SCATTERS[n]:
                 scatter(first, last, n)

@@ -18,24 +18,23 @@ ACT = mybir.ActivationFunctionType
 
 P = 128
 PACK = 4
-KP = P * PACK
-A_PASSES = K // KP
-B_BLOCKS = H // KP
-N_TILES = N // P
-CH = 256
-CHUNKS = S // CH
+PASS = P * PACK
+K_PASSES = K // PASS
+GROUPS = H // PASS
+ROW_TILES = N // P
+CHUNK = 256
+CHUNKS = S // CHUNK
+LIST_ROWS = 16
+QUADRANTS = 4
 TINY = 1e-30
 
-UNIT_ORDER = [(0, 0), (1, 0), (0, 1), (1, 1), (0, 2), (1, 2), (2, 0), (2, 1), (2, 2), (3, 0), (3, 1), (3, 2)]
-SCATTERS = [[(0, 1), (1, 2), (2, 3), (3, 4)]] * 3 + [[(0, 1), (1, 2), (2, 4)]]
-SCALAR_CASTS = [(0, 0)]
-PROJECT_AFTER = {
-    (0, 2): [(0, [0, 1, 2, 3])],
-    (2, 1): [(1, [0, 1, 2, 3])],
-    (3, 1): [(2, [0, 1])],
-    (3, 2): [(2, [2, 3]), (3, [0, 1, 2, 3])],
-}
-VECTOR_RELU = [(0, 2), (1, 2)]
+UNITS = [(0, 0), (0, 1), (1, 0), (0, 2), (1, 1), (1, 2)] + [(c, g) for c in range(2, CHUNKS) for g in range(GROUPS)]
+PROJECT_AFTER = {(0, 2): [0], (2, 2): [1], (3, 2): [2, 3]}
+SCALAR_CASTS = [(0, 0, 0), (0, 0, 1), (0, 1, 0), (1, 0, 1)]
+VECTOR_RELU = [(0, 0), (1, 1), (1, 2)]
+HALVED_UNITS = [(0, 0), (0, 2)]
+LATE_Y = [(2, 1), (2, 2)]
+SCATTER_RUNS = [[(c, c + 1) for c in range(CHUNKS)]] * (ROW_TILES - 1) + [[(0, 1), (1, 2), (2, 4)]]
 
 
 def tile_list_paged_relu2_compact_kernel(
@@ -44,186 +43,203 @@ def tile_list_paged_relu2_compact_kernel(
     nc = tc.nc
     with ExitStack() as ctx:
         keep = ctx.enter_context(tc.tile_pool(name="keep", bufs=1))
-        ring = ctx.enter_context(tc.tile_pool(name="ring", bufs=3))
-        psum_a = ctx.enter_context(tc.psum_pool(name="psum_a", bufs=6))
-        psum_y = ctx.enter_context(tc.psum_pool(name="psum_y", bufs=2))
+        cast_ring = ctx.enter_context(tc.tile_pool(name="cast_ring", bufs=3))
+        relu_ring = ctx.enter_context(tc.tile_pool(name="relu_ring", bufs=4))
+        psum_a = ctx.enter_context(tc.psum_pool(name="psum_a", bufs=4))
+        psum_y = ctx.enter_context(tc.psum_pool(name="psum_y", bufs=4))
 
-        offs_sb = keep.tile([P, S // 16], U16, name="offs_sb")
+        offs_sb = keep.tile([P, S // LIST_ROWS], U16, name="offs_sb")
         nc.sync.dma_start(offs_sb[:], offs)
-        gain_sb = keep.tile([P, B_BLOCKS, PACK], F32, name="gain_sb", tag="vector")
-        nc.sync.dma_start(gain_sb[:], gain.rearrange("(b p t) -> p b t", p=P, t=PACK))
-
-        offs2_sb = keep.tile([P, S // 16], U16, name="offs2_sb")
+        gain_sb = keep.tile([P, GROUPS, PACK], F32, name="gain_sb", tag="vectors")
+        nc.sync.dma_start(gain_sb[:], gain.rearrange("(g p t) -> p g t", p=P, t=PACK))
+        offs2_sb = keep.tile([P, S // LIST_ROWS], U16, name="offs2_sb")
         nc.sync.dma_start(offs2_sb[:], offs2)
-        tsc = keep.tile([P, T // 4], I32, name="tsc", tag="planes", align_bytes=64)
-        nc.vector.memset(tsc[:], 0)
-        tsc_hbm = tab_scales.bitcast(I32)
-        for q in range(4):
-            nc.sync.dma_start(tsc[32 * q : 32 * q + 8, :], tsc_hbm[:, 4 * q : 4 * q + 4, :])
 
-        tabw = []
-        for a in range(A_PASSES):
-            tw = keep.tile([P, T], I32, name="tabw%d" % a, tag="big%d" % a, align_bytes=64)
-            nc.sync.dma_start(tw[:], tab_words[a].rearrange("p t i -> p (t i)").bitcast(I32))
-            tabw.append(tw)
+        tab_scale_sb = keep.tile([P, T // 4], I32, name="tab_scale_sb", tag="scale_rows", align_bytes=64)
+        nc.vector.memset(tab_scale_sb[:], 0)
+        tab_scale_hbm = tab_scales.bitcast(I32)
+        for q in range(QUADRANTS):
+            nc.sync.dma_start(tab_scale_sb[32 * q : 32 * q + 8, :], tab_scale_hbm[:, 4 * q : 4 * q + 4, :])
 
-        raw = {}
+        tab_word_sb = []
+        for a in range(K_PASSES):
+            words = keep.tile([P, T], I32, name="tab_word%d" % a, tag="big%d" % a, align_bytes=64)
+            nc.sync.dma_start(words[:], tab_words[a].rearrange("p t i -> p (t i)").bitcast(I32))
+            tab_word_sb.append(words)
 
-        def load_w1(b, a, dst):
-            nc.sync.dma_start(
-                dst, w1[KP * a : KP * (a + 1), KP * b : KP * (b + 1)].rearrange("(p j) c -> p j c", j=PACK)
-            )
-            raw[b, a] = dst
+        w1_raw = {}
 
-        for a in range(A_PASSES):
-            rw = keep.tile([P, PACK, KP], F32, name="raw0%d" % a, tag="first%d" % a, align_bytes=64)
-            load_w1(0, a, rw[:])
+        def load_w1(g, a, dst):
+            rows = w1[PASS * a : PASS * (a + 1), PASS * g : PASS * (g + 1)]
+            nc.sync.dma_start(dst, rows.rearrange("(p j) c -> p j c", j=PACK))
+            w1_raw[g, a] = dst
 
-        g = gain_sb[:].rearrange("p b t -> p (b t)")
-        width = B_BLOCKS * PACK
-        mag = keep.tile([P, width], F32, name="mag")
-        nc.vector.scalar_tensor_tensor(mag[:], g, -1.0, g, ALU.mult, ALU.max)
-        magc = keep.tile([P, width], F32, name="magc")
-        nc.vector.tensor_scalar(magc[:], mag[:], TINY, None, ALU.max)
+        for a in range(K_PASSES):
+            piece = keep.tile([P, PACK, PASS], F32, name="w1_raw0%d" % a, tag="first%d" % a, align_bytes=64)
+            load_w1(0, a, piece[:])
+
+        gain_flat = gain_sb[:].rearrange("p g t -> p (g t)")
+        width = GROUPS * PACK
+        size = keep.tile([P, width], F32, name="size")
+        nc.vector.scalar_tensor_tensor(size[:], gain_flat, -1.0, gain_flat, ALU.mult, ALU.max)
+        floored = keep.tile([P, width], F32, name="floored")
+        nc.vector.tensor_scalar(floored[:], size[:], TINY, None, ALU.max)
         root0 = keep.tile([P, width], F32, name="root0")
-        nc.scalar.activation(root0[:], magc[:], ACT.Sqrt)
-        pos = keep.tile([P, width], F32, name="pos")
-        nc.vector.tensor_scalar(pos[:], g, 0.0, None, ALU.is_gt)
-        neg = keep.tile([P, width], F32, name="neg")
-        nc.vector.tensor_scalar(neg[:], g, 0.0, None, ALU.is_lt)
-        sgn = keep.tile([P, B_BLOCKS, PACK], BF16, name="sgn")
-        nc.vector.tensor_tensor(sgn[:].rearrange("p b t -> p (b t)"), pos[:], neg[:], ALU.subtract)
-        rec = keep.tile([P, width], F32, name="rec")
-        nc.vector.reciprocal(rec[:], root0[:])
-        quot = keep.tile([P, width], F32, name="quot")
-        nc.vector.tensor_tensor(quot[:], magc[:], rec[:], ALU.mult)
-        both = keep.tile([P, width], F32, name="both")
-        nc.vector.tensor_tensor(both[:], quot[:], root0[:], ALU.add)
+        nc.scalar.activation(root0[:], floored[:], ACT.Sqrt)
+        positive = keep.tile([P, width], F32, name="positive")
+        nc.vector.tensor_scalar(positive[:], gain_flat, 0.0, None, ALU.is_gt)
+        negative = keep.tile([P, width], F32, name="negative")
+        nc.vector.tensor_scalar(negative[:], gain_flat, 0.0, None, ALU.is_lt)
+        sign = keep.tile([P, GROUPS, PACK], BF16, name="sign")
+        nc.vector.tensor_tensor(sign[:].rearrange("p g t -> p (g t)"), positive[:], negative[:], ALU.subtract)
+        inverse = keep.tile([P, width], F32, name="inverse")
+        nc.vector.reciprocal(inverse[:], root0[:])
+        quotient = keep.tile([P, width], F32, name="quotient")
+        nc.vector.tensor_tensor(quotient[:], floored[:], inverse[:], ALU.mult)
+        twice_root = keep.tile([P, width], F32, name="twice_root")
+        nc.vector.tensor_tensor(twice_root[:], quotient[:], root0[:], ALU.add)
         root = keep.tile([P, width], F32, name="root")
-        nc.vector.tensor_scalar(root[:], both[:], 0.5, None, ALU.mult)
+        nc.vector.tensor_scalar(root[:], twice_root[:], 0.5, None, ALU.mult)
 
         slots = []
-        for n in range(N_TILES):
-            sl = keep.tile([P, T2], F32, name="slots%d" % n)
-            nc.vector.memset(sl[:], 0.0)
-            slots.append(sl)
+        for n in range(ROW_TILES):
+            rows_out = keep.tile([P, T2], F32, name="slots%d" % n)
+            nc.vector.memset(rows_out[:], 0.0)
+            slots.append(rows_out)
 
-        vs = keep.tile([P, S], U8, name="vs", align_bytes=64)
-        nc.vector.tensor_copy(vs[:], tsc[:].bitcast(U8).indirect(offs_sb[:]))
-        vw = []
-        for a in range(A_PASSES):
-            gw = keep.tile([P, S], U32, name="vw%d" % a, align_bytes=64)
-            nc.vector.tensor_copy(gw[:], tabw[a][:].bitcast(U32).indirect(offs_sb[:]))
-            vw.append(gw)
+        v_scales = keep.tile([P, S], U8, name="v_scales", align_bytes=64)
+        nc.vector.tensor_copy(v_scales[:], tab_scale_sb[:].bitcast(U8).indirect(offs_sb[:]))
+        v_words = []
+        for a in range(K_PASSES):
+            picked = keep.tile([P, S], U32, name="v_words%d" % a, align_bytes=64)
+            nc.vector.tensor_copy(picked[:], tab_word_sb[a][:].bitcast(U32).indirect(offs_sb[:]))
+            v_words.append(picked)
 
-        for b in range(1, B_BLOCKS):
-            rw = keep.tile([P, A_PASSES, PACK, KP], F32, name="raw%d" % b, tag="big%d" % (b - 1), align_bytes=64)
-            for a in range(A_PASSES):
-                load_w1(b, a, rw[:, a])
-        w2s = keep.tile([P, B_BLOCKS, N], U8, name="w2s", tag="planes", align_bytes=64)
-        nc.vector.memset(w2s[:].bitcast(I32), 0)
-        w2s_hbm = w2_scales.bitcast(I32).rearrange("b q c -> q b c")
-        for q in range(4):
-            nc.sync.dma_start(w2s[32 * q : 32 * q + 4].bitcast(I32), w2s_hbm[4 * q : 4 * q + 4])
-        b2_sb = keep.tile([P, N_TILES], F32, name="b2_sb", tag="vector")
-        with nc.allow_non_contiguous_dma(reason="one bias a partition"):
-            nc.sync.dma_start(b2_sb[:], b2.rearrange("(c p) -> p c", p=P))
+        for g in range(1, GROUPS):
+            pieces = keep.tile(
+                [P, K_PASSES, PACK, PASS], F32, name="w1_raw%d" % g, tag="big%d" % (g - 1), align_bytes=64
+            )
+            for a in range(K_PASSES):
+                load_w1(g, a, pieces[:, a])
+        w2_scale_sb = keep.tile([P, GROUPS, N], U8, name="w2_scale_sb", tag="scale_rows", align_bytes=64)
+        nc.vector.memset(w2_scale_sb[:].bitcast(I32), 0)
+        w2_scale_hbm = w2_scales.bitcast(I32).rearrange("g q c -> q g c")
+        for q in range(QUADRANTS):
+            nc.sync.dma_start(w2_scale_sb[32 * q : 32 * q + 4].bitcast(I32), w2_scale_hbm[4 * q : 4 * q + 4])
+        b2_sb = keep.tile([P, ROW_TILES], F32, name="b2_sb", tag="vectors")
+        with nc.allow_non_contiguous_dma(reason="one bias value for each partition and row tile"):
+            nc.sync.dma_start(b2_sb[:], b2.rearrange("(n p) -> p n", p=P))
 
-        w1c, w1s = {}, {}
-        for b in range(B_BLOCKS):
-            for a in range(A_PASSES):
-                wb = ring.tile([P, PACK * KP], BF16, name="wb", align_bytes=64, bufs=2)
-                dst = wb[:].rearrange("p (t m j) -> p m j t", t=PACK, j=PACK)
-                src = raw[b, a].rearrange("p j (m t) -> p m j t", t=PACK)
-                for t in range(0, PACK, 2):
-                    if (b, a) in SCALAR_CASTS:
-                        nc.scalar.copy(dst[:, :, :, t : t + 2], src[:, :, :, t : t + 2])
+        w1_words, w1_scales = {}, {}
+        for g in range(GROUPS):
+            for a in range(K_PASSES):
+                rounded = cast_ring.tile([P, PACK * PASS], BF16, name="rounded", align_bytes=64)
+                dst = rounded[:].rearrange("p (t m j) -> p m j t", t=PACK, j=PACK)
+                src = w1_raw[g, a].rearrange("p j (m t) -> p m j t", t=PACK)
+                for half in range(2):
+                    pair = slice(2 * half, 2 * half + 2)
+                    if (g, a, half) in SCALAR_CASTS:
+                        nc.scalar.copy(dst[:, :, :, pair], src[:, :, :, pair])
                     else:
-                        nc.vector.tensor_copy(dst[:, :, :, t : t + 2], src[:, :, :, t : t + 2])
-                wc = keep.tile([P, KP], U32, name="w1c%d%d" % (b, a), align_bytes=64)
-                ws = keep.tile([P, KP], U8, name="w1s%d%d" % (b, a), align_bytes=64)
-                nc.vector.quantize_mx(out=wc[:].bitcast(FP8X4), scales=ws[:], in_=wb[:])
-                w1c[b, a], w1s[b, a] = wc, ws
+                        nc.vector.tensor_copy(dst[:, :, :, pair], src[:, :, :, pair])
+                codes = keep.tile([P, PASS], U32, name="w1_words%d%d" % (g, a), align_bytes=64)
+                scales = keep.tile([P, PASS], U8, name="w1_scales%d%d" % (g, a), align_bytes=64)
+                for half in range(2):
+                    cols = slice(PASS // 2 * half, PASS // 2 * (half + 1))
+                    nc.vector.quantize_mx(
+                        out=codes[:, cols].bitcast(FP8X4),
+                        scales=scales[:, cols],
+                        in_=rounded[:, PACK * cols.start : PACK * cols.stop],
+                    )
+                w1_words[g, a], w1_scales[g, a] = codes, scales
 
-        w2w = keep.tile([P, B_BLOCKS, 2 * N], U8, name="w2w", tag="first0", align_bytes=64)
-        nc.sync.dma_start(w2w[:].bitcast(I32), w2_words.bitcast(I32).rearrange("b p c -> p b c"))
+        w2_word_sb = keep.tile([P, GROUPS, 2 * N], U8, name="w2_word_sb", tag="first0", align_bytes=64)
+        nc.sync.dma_start(w2_word_sb[:].bitcast(I32), w2_words.bitcast(I32).rearrange("g p c -> p g c"))
         wgo_sb = keep.tile([P, S], F32, name="wgo_sb", tag="first1", align_bytes=64)
         nc.sync.dma_start(wgo_sb[:], wgo)
 
-        hc, hs = {}, {}
-        ysb = [keep.tile([P, S], F32, name="y%d" % n) for n in range(N_TILES)]
+        h_words, h_scales, y_late = {}, {}, {}
+        y_sb = [keep.tile([P, S], F32, name="y%d" % n) for n in range(ROW_TILES)]
 
-        def hidden(c, b):
-            cols = slice(CH * c, CH * (c + 1))
-            r = ring.tile([P, PACK, CH], F32, name="r")
-            for half in range(2):
-                acc = psum_a.tile([P, 2, CH], F32, name="acc")
+        def hidden_unit(c, g):
+            tokens = slice(CHUNK * c, CHUNK * (c + 1))
+            if (c, g) == UNITS[-1]:
+                rectified = keep.tile([P, PACK, CHUNK], F32, name="rectified_last", tag="late")
+            else:
+                rectified = relu_ring.tile([P, PACK, CHUNK], F32, name="rectified")
+            for bank in range(2):
+                acc = psum_a.tile([P, 2, CHUNK], F32, name="acc")
                 for u in range(2):
-                    t = 2 * half + u
-                    m = slice(P * t, P * (t + 1))
-                    for a in range(A_PASSES):
+                    cols = slice(P * (2 * bank + u), P * (2 * bank + u + 1))
+                    for a in range(K_PASSES):
                         nc.tensor.matmul_mx(
                             out=acc[:, u, :],
-                            lhsT=w1c[b, a][:, m].bitcast(FP8X4),
-                            lhsT_scale=w1s[b, a][:, m],
-                            rhs=vw[a][:, cols].bitcast(FP8X4),
-                            rhs_scale=vs[4 * a :, cols],
+                            lhsT=w1_words[g, a][:, cols].bitcast(FP8X4),
+                            lhsT_scale=w1_scales[g, a][:, cols],
+                            rhs=v_words[a][:, tokens].bitcast(FP8X4),
+                            rhs_scale=v_scales[4 * a :, tokens],
                             start=(a == 0),
-                            stop=(a == A_PASSES - 1),
+                            stop=(a == K_PASSES - 1),
                         )
                 for u in range(2):
-                    t = 2 * half + u
-                    s = root[:, PACK * b + t : PACK * b + t + 1]
-                    if half == 1 and (c, b) in VECTOR_RELU:
-                        nc.vector.tensor_scalar(r[:, t, :], acc[:, u, :], 0.0, s, ALU.max, ALU.mult)
+                    t = 2 * bank + u
+                    factor = root[:, PACK * g + t : PACK * g + t + 1]
+                    if bank == 1 and (c, g) in VECTOR_RELU:
+                        nc.vector.tensor_scalar(rectified[:, t, :], acc[:, u, :], 0.0, factor, ALU.max, ALU.mult)
                     else:
-                        nc.scalar.activation(r[:, t, :], acc[:, u, :], ACT.Relu, scale=s)
-            sq = keep.tile([P, CH * PACK], BF16, name="sq%d%d" % (c, b), align_bytes=64)
-            nc.scalar.activation(
-                sq[:].rearrange("p (c t) -> p c t", t=PACK),
-                r[:].rearrange("p t c -> p c t"),
-                ACT.Square,
-            )
-            nc.vector.tensor_tensor(
-                sq[:].rearrange("p (c t) -> p c t", t=PACK),
-                sq[:].rearrange("p (c t) -> p c t", t=PACK),
-                sgn[:, b : b + 1, :].to_broadcast([P, CH, PACK]),
-                ALU.mult,
-            )
-            codes = keep.tile([P, CH], U32, name="hc%d%d" % (c, b), align_bytes=64)
-            scales = keep.tile([P, CH], U8, name="hs%d%d" % (c, b), align_bytes=64)
-            nc.vector.quantize_mx(out=codes[:].bitcast(FP8X4), scales=scales[:], in_=sq[:])
-            hc[c, b], hs[c, b] = codes, scales
-
-        def project(c, tiles):
-            for n in tiles:
-                acc = psum_y.tile([P, CH], F32, name="yacc")
-                for h in range(CH // P):
-                    cols = slice(P * h, P * (h + 1))
-                    for b in range(B_BLOCKS):
-                        nc.tensor.matmul_mx(
-                            out=acc[:, cols],
-                            lhsT=w2w[:, b, 2 * P * n : 2 * P * (n + 1)].bitcast(FP4X4),
-                            lhsT_scale=w2s[:, b, P * n : P * (n + 1)],
-                            rhs=hc[c, b][:, cols].bitcast(FP8X4),
-                            rhs_scale=hs[c, b][:, cols],
-                            start=(b == 0),
-                            stop=(b == B_BLOCKS - 1),
-                        )
+                        nc.scalar.activation(rectified[:, t, :], acc[:, u, :], ACT.Relu, scale=factor)
+            h = keep.tile([P, CHUNK * PACK], BF16, name="h%d%d" % (c, g), align_bytes=64)
+            codes = keep.tile([P, CHUNK], U32, name="h_words%d%d" % (c, g), align_bytes=64)
+            scales = keep.tile([P, CHUNK], U8, name="h_scales%d%d" % (c, g), align_bytes=64)
+            step = CHUNK // 2 if (c, g) in HALVED_UNITS else CHUNK
+            parts = [slice(x, x + step) for x in range(0, CHUNK, step)]
+            h_by_token = h[:].rearrange("p (c t) -> p c t", t=PACK)
+            for part in parts:
                 nc.scalar.activation(
-                    ysb[n][:, CH * c : CH * (c + 1)], acc[:], ACT.Identity, bias=b2_sb[:, n : n + 1]
+                    h_by_token[:, part], rectified[:, :, part].rearrange("p t c -> p c t"), ACT.Square
                 )
+            for part in parts:
+                signs = sign[:, g : g + 1, :].to_broadcast([P, step, PACK])
+                nc.vector.tensor_tensor(h_by_token[:, part], h_by_token[:, part], signs, ALU.mult)
+            for part in parts:
+                nc.vector.quantize_mx(
+                    out=codes[:, part].bitcast(FP8X4),
+                    scales=scales[:, part],
+                    in_=h[:, PACK * part.start : PACK * part.stop],
+                )
+            h_words[c, g], h_scales[c, g] = codes, scales
 
-        def scatter(first, last, n):
-            places = offs2_sb[:, CH // 16 * first : CH // 16 * last]
-            cols = slice(CH * first, CH * last)
-            nc.vector.tensor_tensor(slots[n][:].indirect(places), ysb[n][:, cols], wgo_sb[:, cols], ALU.mult)
+        def project(c):
+            for n in range(ROW_TILES):
+                y_acc = psum_y.tile([P, CHUNK], F32, name="y_acc")
+                for first in range(0, CHUNK, P):
+                    part = slice(first, first + P)
+                    for g in range(GROUPS):
+                        nc.tensor.matmul_mx(
+                            out=y_acc[:, part],
+                            lhsT=w2_word_sb[:, g, 2 * P * n : 2 * P * (n + 1)].bitcast(FP4X4),
+                            lhsT_scale=w2_scale_sb[:, g, P * n : P * (n + 1)],
+                            rhs=h_words[c, g][:, part].bitcast(FP8X4),
+                            rhs_scale=h_scales[c, g][:, part],
+                            start=(g == 0),
+                            stop=(g == GROUPS - 1),
+                        )
+                if (c, n) == LATE_Y[0]:
+                    late = keep.tile([P, len(LATE_Y), CHUNK], F32, name="y_late", tag="late")
+                    for place, key in enumerate(LATE_Y):
+                        y_late[key] = late[:, place, :]
+                dst = y_late.get((c, n), y_sb[n][:, CHUNK * c : CHUNK * (c + 1)])
+                nc.scalar.activation(dst, y_acc[:], ACT.Identity, bias=b2_sb[:, n : n + 1])
 
-        for c, b in UNIT_ORDER:
-            hidden(c, b)
-            for chunk, tiles in PROJECT_AFTER.get((c, b), []):
-                project(chunk, tiles)
-        for n in range(N_TILES):
-            for first, last in SCATTERS[n]:
-                scatter(first, last, n)
+        for c, g in UNITS:
+            hidden_unit(c, g)
+            for chunk in PROJECT_AFTER.get((c, g), []):
+                project(chunk)
+
+        for n in range(ROW_TILES):
+            for first, last in SCATTER_RUNS[n]:
+                places = offs2_sb[:, CHUNK // LIST_ROWS * first : CHUNK // LIST_ROWS * last]
+                tokens = slice(CHUNK * first, CHUNK * last)
+                values = y_late.get((first, n), y_sb[n][:, tokens])
+                nc.vector.tensor_tensor(slots[n][:].indirect(places), values, wgo_sb[:, tokens], ALU.mult)
             nc.sync.dma_start(out[P * n : P * (n + 1), :], slots[n][:])

@@ -25,16 +25,16 @@ ROW_TILES = N // P
 CHUNK = 256
 CHUNKS = S // CHUNK
 LIST_ROWS = 16
+BANK = 512
 QUADRANTS = 4
 TINY = 1e-30
 
-UNITS = [(0, 0), (0, 1), (1, 0), (0, 2), (1, 1), (1, 2)] + [(c, g) for c in range(2, CHUNKS) for g in range(GROUPS)]
-PROJECT_AFTER = {(0, 2): [0], (2, 2): [1], (3, 2): [2, 3]}
-SCALAR_CASTS = [(0, 0, 0), (0, 0, 1), (0, 1, 0), (1, 0, 1)]
-VECTOR_RELU = [(0, 0), (1, 1), (1, 2)]
-HALVED_UNITS = [(0, 0), (0, 2)]
-LATE_Y = [(2, 1), (2, 2)]
-SCATTER_RUNS = [[(c, c + 1) for c in range(CHUNKS)]] * (ROW_TILES - 1) + [[(0, 1), (1, 2), (2, 4)]]
+SCALAR_CASTS = [(0, 0, 0), (0, 0, 1), (0, 1, 1)]
+LAST_PIECE = None
+GORDER = (2, 0, 1)
+SCALAR_MOVES = 6
+SCATTER_RUNS = [(n, c, c + 1) for c in range(2) for n in range(ROW_TILES)]
+SCATTER_RUNS = SCATTER_RUNS + [(0, 2, 3), (1, 2, 3), (0, 3, 4), (1, 3, 4), (2, 2, 4), (3, 2, 4)]
 
 
 def tile_list_paged_relu2_compact_kernel(
@@ -44,34 +44,37 @@ def tile_list_paged_relu2_compact_kernel(
     with ExitStack() as ctx:
         keep = ctx.enter_context(tc.tile_pool(name="keep", bufs=1))
         cast_ring = ctx.enter_context(tc.tile_pool(name="cast_ring", bufs=3))
-        relu_ring = ctx.enter_context(tc.tile_pool(name="relu_ring", bufs=4))
         psum_a = ctx.enter_context(tc.psum_pool(name="psum_a", bufs=4))
         psum_y = ctx.enter_context(tc.psum_pool(name="psum_y", bufs=4))
 
         offs_sb = keep.tile([P, S // LIST_ROWS], U16, name="offs_sb")
         nc.sync.dma_start(offs_sb[:], offs)
-        gain_sb = keep.tile([P, GROUPS, PACK], F32, name="gain_sb", tag="vectors")
-        nc.sync.dma_start(gain_sb[:], gain.rearrange("(g p t) -> p g t", p=P, t=PACK))
-        offs2_sb = keep.tile([P, S // LIST_ROWS], U16, name="offs2_sb")
-        nc.sync.dma_start(offs2_sb[:], offs2)
-
-        tab_scale_sb = keep.tile([P, T // 4], I32, name="tab_scale_sb", tag="scale_rows", align_bytes=64)
-        nc.vector.memset(tab_scale_sb[:], 0)
-        tab_scale_hbm = tab_scales.bitcast(I32)
-        for q in range(QUADRANTS):
-            nc.sync.dma_start(tab_scale_sb[32 * q : 32 * q + 8, :], tab_scale_hbm[:, 4 * q : 4 * q + 4, :])
-
         tab_word_sb = []
-        for a in range(K_PASSES):
+
+        def load_table(a):
             words = keep.tile([P, T], I32, name="tab_word%d" % a, tag="big%d" % a, align_bytes=64)
             nc.sync.dma_start(words[:], tab_words[a].rearrange("p t i -> p (t i)").bitcast(I32))
             tab_word_sb.append(words)
+
+        tab_scale_sb = keep.tile([P, T // 4], I32, name="tab_scale_sb", align_bytes=64)
+        nc.sync.dma_start(tab_scale_sb[:32, :], tab_scales.bitcast(I32).rearrange("a q t -> (a q) t"))
+        nc.vector.memset(tab_scale_sb[32:64, :], 0)
+        nc.vector.memset(tab_scale_sb[64:, :], 0)
+        gain_sb = keep.tile([P, GROUPS, PACK], F32, name="gain_sb")
+        nc.sync.dma_start(gain_sb[:], gain.rearrange("(g p t) -> p g t", p=P, t=PACK))
+        offs2_sb = keep.tile([P, S // LIST_ROWS], U16, name="offs2_sb")
+        nc.sync.dma_start(offs2_sb[:], offs2)
+        for a in range(K_PASSES):
+            load_table(a)
 
         w1_raw = {}
 
         def load_w1(g, a, dst):
             rows = w1[PASS * a : PASS * (a + 1), PASS * g : PASS * (g + 1)]
-            nc.sync.dma_start(dst, rows.rearrange("(p j) c -> p j c", j=PACK))
+            src = rows.rearrange("(p j) c -> p j c", j=PACK)
+            step = PASS // 2 if (g, a) == LAST_PIECE else PASS
+            for first in range(0, PASS, step):
+                nc.sync.dma_start(dst[:, :, first : first + step], src[:, :, first : first + step])
             w1_raw[g, a] = dst
 
         for a in range(K_PASSES):
@@ -101,19 +104,26 @@ def tile_list_paged_relu2_compact_kernel(
         root = keep.tile([P, width], F32, name="root")
         nc.vector.tensor_scalar(root[:], twice_root[:], 0.5, None, ALU.mult)
 
-        slots = []
-        for n in range(ROW_TILES):
-            rows_out = keep.tile([P, T2], F32, name="slots%d" % n)
-            nc.vector.memset(rows_out[:], 0.0)
-            slots.append(rows_out)
-
+        picked_scales = keep.tile([P, S], U8, name="picked_scales", align_bytes=64)
+        nc.vector.tensor_copy(picked_scales[:], tab_scale_sb[:].bitcast(U8).indirect(offs_sb[:]))
         v_scales = keep.tile([P, S], U8, name="v_scales", align_bytes=64)
-        nc.vector.tensor_copy(v_scales[:], tab_scale_sb[:].bitcast(U8).indirect(offs_sb[:]))
+        nc.vector.memset(v_scales[:].bitcast(I32), 0)
+        moves = [(a, i) for a in range(K_PASSES) for i in range(4)]
+        for place, (a, i) in enumerate(moves):
+            queue = nc.scalar if place < SCALAR_MOVES else nc.gpsimd
+            src = picked_scales[16 * a + i : 16 * (a + 1) : 4]
+            queue.dma_start(v_scales[4 * a + i : P : 32].bitcast(I32), src.bitcast(I32))
         v_words = []
         for a in range(K_PASSES):
             picked = keep.tile([P, S], U32, name="v_words%d" % a, align_bytes=64)
             nc.vector.tensor_copy(picked[:], tab_word_sb[a][:].bitcast(U32).indirect(offs_sb[:]))
             v_words.append(picked)
+
+        slots = []
+        for n in range(ROW_TILES):
+            rows_out = keep.tile([P, T2], F32, name="slots%d" % n)
+            nc.gpsimd.memset(rows_out[:], 0.0)
+            slots.append(rows_out)
 
         for g in range(1, GROUPS):
             pieces = keep.tile(
@@ -121,83 +131,101 @@ def tile_list_paged_relu2_compact_kernel(
             )
             for a in range(K_PASSES):
                 load_w1(g, a, pieces[:, a])
-        w2_scale_sb = keep.tile([P, GROUPS, N], U8, name="w2_scale_sb", tag="scale_rows", align_bytes=64)
-        nc.vector.memset(w2_scale_sb[:].bitcast(I32), 0)
-        w2_scale_hbm = w2_scales.bitcast(I32).rearrange("g q c -> q g c")
-        for q in range(QUADRANTS):
-            nc.sync.dma_start(w2_scale_sb[32 * q : 32 * q + 4].bitcast(I32), w2_scale_hbm[4 * q : 4 * q + 4])
-        b2_sb = keep.tile([P, ROW_TILES], F32, name="b2_sb", tag="vectors")
-        with nc.allow_non_contiguous_dma(reason="one bias value for each partition and row tile"):
-            nc.sync.dma_start(b2_sb[:], b2.rearrange("(n p) -> p n", p=P))
 
         w1_words, w1_scales = {}, {}
-        for g in range(GROUPS):
-            for a in range(K_PASSES):
+
+        def quantise_w1(g, a):
+            if g == 0:
+                rounded = keep.tile([P, PACK * PASS], BF16, name="r0%d" % a, tag="r0%d" % a, align_bytes=64)
+            else:
                 rounded = cast_ring.tile([P, PACK * PASS], BF16, name="rounded", align_bytes=64)
-                dst = rounded[:].rearrange("p (t m j) -> p m j t", t=PACK, j=PACK)
-                src = w1_raw[g, a].rearrange("p j (m t) -> p m j t", t=PACK)
-                for half in range(2):
-                    pair = slice(2 * half, 2 * half + 2)
-                    if (g, a, half) in SCALAR_CASTS:
-                        nc.scalar.copy(dst[:, :, :, pair], src[:, :, :, pair])
-                    else:
-                        nc.vector.tensor_copy(dst[:, :, :, pair], src[:, :, :, pair])
-                codes = keep.tile([P, PASS], U32, name="w1_words%d%d" % (g, a), align_bytes=64)
-                scales = keep.tile([P, PASS], U8, name="w1_scales%d%d" % (g, a), align_bytes=64)
-                for half in range(2):
-                    cols = slice(PASS // 2 * half, PASS // 2 * (half + 1))
-                    nc.vector.quantize_mx(
-                        out=codes[:, cols].bitcast(FP8X4),
-                        scales=scales[:, cols],
-                        in_=rounded[:, PACK * cols.start : PACK * cols.stop],
-                    )
-                w1_words[g, a], w1_scales[g, a] = codes, scales
+            dst = rounded[:].rearrange("p (t m j) -> p m j t", t=PACK, j=PACK)
+            src = w1_raw[g, a].rearrange("p j (m t) -> p m j t", t=PACK)
+            for half in range(2):
+                if (g, a) == LAST_PIECE:
+                    rows = slice(P // 2 * half, P // 2 * (half + 1))
+                    nc.vector.tensor_copy(dst[:, rows], src[:, rows])
+                    continue
+                pair = slice(2 * half, 2 * half + 2)
+                if (g, a, half) in SCALAR_CASTS:
+                    nc.scalar.copy(dst[:, :, :, pair], src[:, :, :, pair])
+                else:
+                    nc.vector.tensor_copy(dst[:, :, :, pair], src[:, :, :, pair])
+            codes = keep.tile([P, PASS], U32, name="w1_words%d%d" % (g, a), align_bytes=64)
+            scales = keep.tile([P, PASS], U8, name="w1_scales%d%d" % (g, a), align_bytes=64)
+            for half in range(2):
+                cols = slice(PASS // 2 * half, PASS // 2 * (half + 1))
+                nc.vector.quantize_mx(
+                    out=codes[:, cols].bitcast(FP8X4),
+                    scales=scales[:, cols],
+                    in_=rounded[:, PACK * cols.start : PACK * cols.stop],
+                )
+            w1_words[g, a], w1_scales[g, a] = codes, scales
+
+        quantise_w1(0, 0)
+        w2_scale_sb = keep.tile([P, GROUPS, N], U8, name="w2_scale_sb", tag="r00", align_bytes=64)
+        nc.vector.memset(w2_scale_sb[:].bitcast(I32), 0)
+        quantise_w1(0, 1)
 
         w2_word_sb = keep.tile([P, GROUPS, 2 * N], U8, name="w2_word_sb", tag="first0", align_bytes=64)
         nc.sync.dma_start(w2_word_sb[:].bitcast(I32), w2_words.bitcast(I32).rearrange("g p c -> p g c"))
+        w2_scale_hbm = w2_scales.bitcast(I32).rearrange("g q c -> q g c")
+        for q in range(QUADRANTS):
+            nc.sync.dma_start(w2_scale_sb[32 * q : 32 * q + 4].bitcast(I32), w2_scale_hbm[4 * q : 4 * q + 4])
+        b2_sb = keep.tile([P, ROW_TILES], F32, name="b2_sb", tag="r01", align_bytes=64)
+        with nc.allow_non_contiguous_dma(reason="one bias value for each partition and row tile"):
+            nc.sync.dma_start(b2_sb[:], b2.rearrange("(n p) -> p n", p=P))
         wgo_sb = keep.tile([P, S], F32, name="wgo_sb", tag="first1", align_bytes=64)
         nc.sync.dma_start(wgo_sb[:], wgo)
 
-        h_words, h_scales, y_late = {}, {}, {}
+        h_words, h_scales, rectified, y_acc, squared = {}, {}, {}, {}, []
         y_sb = [keep.tile([P, S], F32, name="y%d" % n) for n in range(ROW_TILES)]
 
-        def hidden_unit(c, g):
-            tokens = slice(CHUNK * c, CHUNK * (c + 1))
-            if (c, g) == UNITS[-1]:
-                rectified = keep.tile([P, PACK, CHUNK], F32, name="rectified_last", tag="late")
-            else:
-                rectified = relu_ring.tile([P, PACK, CHUNK], F32, name="rectified")
-            for bank in range(2):
-                acc = psum_a.tile([P, 2, CHUNK], F32, name="acc")
-                for u in range(2):
-                    cols = slice(P * (2 * bank + u), P * (2 * bank + u + 1))
-                    for a in range(K_PASSES):
+        def rectify(g, first, count, vector_banks=()):
+            width = CHUNK * count
+            tokens = slice(CHUNK * first, CHUNK * first + width)
+            per_bank = BANK // width
+            tag = "unit%d%d" % (first, g)
+            values = keep.tile([P, PACK, width], F32, name="values%d%d" % (first, g), tag=tag, align_bytes=64)
+            for bank in range(PACK // per_bank):
+                acc = psum_a.tile([P, per_bank, width], F32, name="acc")
+                for a in range(K_PASSES):
+                    for u in range(per_bank):
+                        t = per_bank * bank + u
+                        cols = slice(P * t, P * (t + 1))
                         nc.tensor.matmul_mx(
                             out=acc[:, u, :],
                             lhsT=w1_words[g, a][:, cols].bitcast(FP8X4),
                             lhsT_scale=w1_scales[g, a][:, cols],
                             rhs=v_words[a][:, tokens].bitcast(FP8X4),
                             rhs_scale=v_scales[4 * a :, tokens],
-                            start=(a == 0),
-                            stop=(a == K_PASSES - 1),
+                            start=(a == 0 and u == 0),
+                            stop=(a == K_PASSES - 1 and u == per_bank - 1),
                         )
-                for u in range(2):
-                    t = 2 * bank + u
+                for u in range(per_bank):
+                    t = per_bank * bank + u
                     factor = root[:, PACK * g + t : PACK * g + t + 1]
-                    if bank == 1 and (c, g) in VECTOR_RELU:
-                        nc.vector.tensor_scalar(rectified[:, t, :], acc[:, u, :], 0.0, factor, ALU.max, ALU.mult)
+                    if bank in vector_banks:
+                        nc.vector.tensor_scalar(values[:, t, :], acc[:, u, :], 0.0, factor, ALU.max, ALU.mult)
                     else:
-                        nc.scalar.activation(rectified[:, t, :], acc[:, u, :], ACT.Relu, scale=factor)
-            h = keep.tile([P, CHUNK * PACK], BF16, name="h%d%d" % (c, g), align_bytes=64)
+                        nc.scalar.activation(values[:, t, :], acc[:, u, :], ACT.Relu, scale=factor)
+            for c in range(count):
+                rectified[first + c, g] = values[:, :, CHUNK * c : CHUNK * (c + 1)]
+
+        def quantise(g, c, step=CHUNK, shared=False):
+            tag = "unit%d%d" % squared[-1] if squared else "h_first"
+            squared.append((c, g))
+            h = keep.tile([P, CHUNK * PACK], BF16, name="h%d%d" % (c, g), tag=tag, align_bytes=64)
             codes = keep.tile([P, CHUNK], U32, name="h_words%d%d" % (c, g), align_bytes=64)
             scales = keep.tile([P, CHUNK], U8, name="h_scales%d%d" % (c, g), align_bytes=64)
-            step = CHUNK // 2 if (c, g) in HALVED_UNITS else CHUNK
             parts = [slice(x, x + step) for x in range(0, CHUNK, step)]
             h_by_token = h[:].rearrange("p (c t) -> p c t", t=PACK)
             for part in parts:
-                nc.scalar.activation(
-                    h_by_token[:, part], rectified[:, :, part].rearrange("p t c -> p c t"), ACT.Square
-                )
+                values = rectified[c, g][:, :, part].rearrange("p t c -> p c t")
+                if shared and part.start == 0:
+                    nc.vector.tensor_tensor(h_by_token[:, part], values, values, ALU.mult)
+                else:
+                    nc.scalar.activation(h_by_token[:, part], values, ACT.Square)
             for part in parts:
                 signs = sign[:, g : g + 1, :].to_broadcast([P, step, PACK])
                 nc.vector.tensor_tensor(h_by_token[:, part], h_by_token[:, part], signs, ALU.mult)
@@ -211,35 +239,77 @@ def tile_list_paged_relu2_compact_kernel(
 
         def project(c):
             for n in range(ROW_TILES):
-                y_acc = psum_y.tile([P, CHUNK], F32, name="y_acc")
-                for first in range(0, CHUNK, P):
+                acc = psum_y.tile([P, CHUNK], F32, name="y_acc")
+                passes = [(g, first) for g in (GORDER if c == 0 else range(GROUPS)) for first in range(0, CHUNK, P)]
+                for g, first in passes:
                     part = slice(first, first + P)
-                    for g in range(GROUPS):
-                        nc.tensor.matmul_mx(
-                            out=y_acc[:, part],
-                            lhsT=w2_word_sb[:, g, 2 * P * n : 2 * P * (n + 1)].bitcast(FP4X4),
-                            lhsT_scale=w2_scale_sb[:, g, P * n : P * (n + 1)],
-                            rhs=h_words[c, g][:, part].bitcast(FP8X4),
-                            rhs_scale=h_scales[c, g][:, part],
-                            start=(g == 0),
-                            stop=(g == GROUPS - 1),
-                        )
-                if (c, n) == LATE_Y[0]:
-                    late = keep.tile([P, len(LATE_Y), CHUNK], F32, name="y_late", tag="late")
-                    for place, key in enumerate(LATE_Y):
-                        y_late[key] = late[:, place, :]
-                dst = y_late.get((c, n), y_sb[n][:, CHUNK * c : CHUNK * (c + 1)])
-                nc.scalar.activation(dst, y_acc[:], ACT.Identity, bias=b2_sb[:, n : n + 1])
+                    nc.tensor.matmul_mx(
+                        out=acc[:, part],
+                        lhsT=w2_word_sb[:, g, 2 * P * n : 2 * P * (n + 1)].bitcast(FP4X4),
+                        lhsT_scale=w2_scale_sb[:, g, P * n : P * (n + 1)],
+                        rhs=h_words[c, g][:, part].bitcast(FP8X4),
+                        rhs_scale=h_scales[c, g][:, part],
+                        start=((g, first) == passes[0]),
+                        stop=((g, first) == passes[-1]),
+                    )
+                y_acc[c, n] = acc
 
-        for c, g in UNITS:
-            hidden_unit(c, g)
-            for chunk in PROJECT_AFTER.get((c, g), []):
-                project(chunk)
+        def add_bias(c, n):
+            dst = y_sb[n][:, CHUNK * c : CHUNK * (c + 1)]
+            nc.scalar.activation(dst, y_acc[c, n][:], ACT.Identity, bias=b2_sb[:, n : n + 1])
 
-        for n in range(ROW_TILES):
-            for first, last in SCATTER_RUNS[n]:
-                places = offs2_sb[:, CHUNK // LIST_ROWS * first : CHUNK // LIST_ROWS * last]
-                tokens = slice(CHUNK * first, CHUNK * last)
-                values = y_late.get((first, n), y_sb[n][:, tokens])
-                nc.vector.tensor_tensor(slots[n][:].indirect(places), values, wgo_sb[:, tokens], ALU.mult)
-            nc.sync.dma_start(out[P * n : P * (n + 1), :], slots[n][:])
+        quantise_w1(1, 0)
+        quantise_w1(1, 1)
+        rectify(0, 0, 1)
+        quantise(0, 0)
+        rectify(0, 1, 1)
+        quantise_w1(2, 0)
+        quantise_w1(2, 1)
+        rectify(1, 0, 1)
+        quantise(1, 0)
+        rectify(1, 1, 1)
+        rectify(0, 2, 1)
+        rectify(2, 0, 1, vector_banks=[1])
+        quantise(2, 0, step=P, shared=True)
+        project(0)
+        add_bias(0, 0)
+        quantise(0, 1)
+        rectify(2, 1, 1)
+        quantise(1, 1)
+        add_bias(0, 1)
+        quantise(2, 1)
+        add_bias(0, 2)
+        project(1)
+        add_bias(0, 3)
+        rectify(1, 2, 1)
+        rectify(2, 2, 1)
+        quantise(0, 2)
+        add_bias(1, 0)
+        quantise(1, 2)
+        add_bias(1, 1)
+        rectify(0, 3, 1)
+        quantise(2, 2)
+        add_bias(1, 2)
+        project(2)
+        add_bias(1, 3)
+        rectify(1, 3, 1)
+        rectify(2, 3, 1)
+        quantise(0, 3)
+        add_bias(2, 2)
+        quantise(1, 3)
+        add_bias(2, 3)
+        quantise(2, 3)
+        add_bias(2, 0)
+        add_bias(2, 1)
+        project(3)
+        add_bias(3, 0)
+        add_bias(3, 1)
+        add_bias(3, 2)
+        add_bias(3, 3)
+
+        for n, first, last in SCATTER_RUNS:
+            places = offs2_sb[:, CHUNK // LIST_ROWS * first : CHUNK // LIST_ROWS * last]
+            tokens = slice(CHUNK * first, CHUNK * last)
+            nc.vector.tensor_tensor(slots[n][:].indirect(places), y_sb[n][:, tokens], wgo_sb[:, tokens], ALU.mult)
+            if last == CHUNKS:
+                nc.sync.dma_start(out[P * n : P * (n + 1), :], slots[n][:])

@@ -31,8 +31,7 @@ TINY = 1e-30
 
 SCALAR_CASTS = [(0, 0, 0), (0, 0, 1), (0, 1, 1)]
 LAST_PIECE = None
-GORDER = (2, 0, 1)
-SCALAR_MOVES = 6
+GORDER = (1, 0, 2)
 SCATTER_RUNS = [(n, c, c + 1) for c in range(2) for n in range(ROW_TILES)]
 SCATTER_RUNS = SCATTER_RUNS + [(0, 2, 3), (1, 2, 3), (0, 3, 4), (1, 3, 4), (2, 2, 4), (3, 2, 4)]
 
@@ -56,16 +55,19 @@ def tile_list_paged_relu2_compact_kernel(
             nc.sync.dma_start(words[:], tab_words[a].rearrange("p t i -> p (t i)").bitcast(I32))
             tab_word_sb.append(words)
 
-        tab_scale_sb = keep.tile([P, T // 4], I32, name="tab_scale_sb", align_bytes=64)
-        nc.sync.dma_start(tab_scale_sb[:32, :], tab_scales.bitcast(I32).rearrange("a q t -> (a q) t"))
-        nc.vector.memset(tab_scale_sb[32:64, :], 0)
-        nc.vector.memset(tab_scale_sb[64:, :], 0)
         gain_sb = keep.tile([P, GROUPS, PACK], F32, name="gain_sb")
         nc.sync.dma_start(gain_sb[:], gain.rearrange("(g p t) -> p g t", p=P, t=PACK))
+        load_table(0)
         offs2_sb = keep.tile([P, S // LIST_ROWS], U16, name="offs2_sb")
         nc.sync.dma_start(offs2_sb[:], offs2)
-        for a in range(K_PASSES):
-            load_table(a)
+
+        tab_scale_sb = keep.tile([P, T // 4], I32, name="tab_scale_sb", align_bytes=64)
+        nc.vector.memset(tab_scale_sb[:], 0)
+        tab_scale_hbm = tab_scales.bitcast(I32)
+        for q in range(QUADRANTS):
+            nc.sync.dma_start(tab_scale_sb[32 * q : 32 * q + 8, :], tab_scale_hbm[:, 4 * q : 4 * q + 4, :])
+
+        load_table(1)
 
         w1_raw = {}
 
@@ -104,15 +106,8 @@ def tile_list_paged_relu2_compact_kernel(
         root = keep.tile([P, width], F32, name="root")
         nc.vector.tensor_scalar(root[:], twice_root[:], 0.5, None, ALU.mult)
 
-        picked_scales = keep.tile([P, S], U8, name="picked_scales", align_bytes=64)
-        nc.vector.tensor_copy(picked_scales[:], tab_scale_sb[:].bitcast(U8).indirect(offs_sb[:]))
         v_scales = keep.tile([P, S], U8, name="v_scales", align_bytes=64)
-        nc.vector.memset(v_scales[:].bitcast(I32), 0)
-        moves = [(a, i) for a in range(K_PASSES) for i in range(4)]
-        for place, (a, i) in enumerate(moves):
-            queue = nc.scalar if place < SCALAR_MOVES else nc.gpsimd
-            src = picked_scales[16 * a + i : 16 * (a + 1) : 4]
-            queue.dma_start(v_scales[4 * a + i : P : 32].bitcast(I32), src.bitcast(I32))
+        nc.vector.tensor_copy(v_scales[:], tab_scale_sb[:].bitcast(U8).indirect(offs_sb[:]))
         v_words = []
         for a in range(K_PASSES):
             picked = keep.tile([P, S], U32, name="v_words%d" % a, align_bytes=64)
@@ -122,7 +117,7 @@ def tile_list_paged_relu2_compact_kernel(
         slots = []
         for n in range(ROW_TILES):
             rows_out = keep.tile([P, T2], F32, name="slots%d" % n)
-            nc.gpsimd.memset(rows_out[:], 0.0)
+            nc.vector.memset(rows_out[:], 0.0)
             slots.append(rows_out)
 
         for g in range(1, GROUPS):
@@ -178,7 +173,7 @@ def tile_list_paged_relu2_compact_kernel(
         wgo_sb = keep.tile([P, S], F32, name="wgo_sb", tag="first1", align_bytes=64)
         nc.sync.dma_start(wgo_sb[:], wgo)
 
-        h_words, h_scales, rectified, y_acc, squared = {}, {}, {}, {}, []
+        h_words, h_scales, rectified, y_acc = {}, {}, {}, {}
         y_sb = [keep.tile([P, S], F32, name="y%d" % n) for n in range(ROW_TILES)]
 
         def rectify(g, first, count, vector_banks=()):
@@ -213,8 +208,7 @@ def tile_list_paged_relu2_compact_kernel(
                 rectified[first + c, g] = values[:, :, CHUNK * c : CHUNK * (c + 1)]
 
         def quantise(g, c, step=CHUNK, shared=False):
-            tag = "unit%d%d" % squared[-1] if squared else "h_first"
-            squared.append((c, g))
+            tag = "h%d%d" % (c % 2, g)
             h = keep.tile([P, CHUNK * PACK], BF16, name="h%d%d" % (c, g), tag=tag, align_bytes=64)
             codes = keep.tile([P, CHUNK], U32, name="h_words%d%d" % (c, g), align_bytes=64)
             scales = keep.tile([P, CHUNK], U8, name="h_scales%d%d" % (c, g), align_bytes=64)
@@ -260,23 +254,21 @@ def tile_list_paged_relu2_compact_kernel(
 
         quantise_w1(1, 0)
         quantise_w1(1, 1)
-        rectify(0, 0, 1)
+        rectify(0, 0, 2)
         quantise(0, 0)
-        rectify(0, 1, 1)
         quantise_w1(2, 0)
         quantise_w1(2, 1)
-        rectify(1, 0, 1)
+        quantise(0, 1)
+        rectify(1, 0, 2)
         quantise(1, 0)
-        rectify(1, 1, 1)
-        rectify(0, 2, 1)
-        rectify(2, 0, 1, vector_banks=[1])
+        rectify(2, 0, 1)
         quantise(2, 0, step=P, shared=True)
+        quantise(1, 1)
         project(0)
         add_bias(0, 0)
-        quantise(0, 1)
-        rectify(2, 1, 1)
-        quantise(1, 1)
         add_bias(0, 1)
+        rectify(2, 1, 1)
+        rectify(0, 2, 2)
         quantise(2, 1)
         add_bias(0, 2)
         project(1)
@@ -287,16 +279,15 @@ def tile_list_paged_relu2_compact_kernel(
         add_bias(1, 0)
         quantise(1, 2)
         add_bias(1, 1)
-        rectify(0, 3, 1)
+        rectify(1, 3, 1)
         quantise(2, 2)
         add_bias(1, 2)
         project(2)
         add_bias(1, 3)
-        rectify(1, 3, 1)
-        rectify(2, 3, 1)
         quantise(0, 3)
-        add_bias(2, 2)
+        rectify(2, 3, 1)
         quantise(1, 3)
+        add_bias(2, 2)
         add_bias(2, 3)
         quantise(2, 3)
         add_bias(2, 0)

@@ -57,17 +57,16 @@ def tile_list_paged_relu2_compact_kernel(
 
         gain_sb = keep.tile([P, GROUPS, PACK], F32, name="gain_sb")
         nc.sync.dma_start(gain_sb[:], gain.rearrange("(g p t) -> p g t", p=P, t=PACK))
-        load_table(0)
         offs2_sb = keep.tile([P, S // LIST_ROWS], U16, name="offs2_sb")
         nc.sync.dma_start(offs2_sb[:], offs2)
 
         tab_scale_sb = keep.tile([P, T // 4], I32, name="tab_scale_sb", align_bytes=64)
         nc.vector.memset(tab_scale_sb[:], 0)
         tab_scale_hbm = tab_scales.bitcast(I32)
-        for q in range(QUADRANTS):
-            nc.sync.dma_start(tab_scale_sb[32 * q : 32 * q + 8, :], tab_scale_hbm[:, 4 * q : 4 * q + 4, :])
-
-        load_table(1)
+        for a in range(K_PASSES):
+            nc.sync.dma_start(tab_scale_sb[4 * a : P : 8, :], tab_scale_hbm[a])
+        for a in range(K_PASSES):
+            load_table(a)
 
         w1_raw = {}
 
@@ -106,8 +105,13 @@ def tile_list_paged_relu2_compact_kernel(
         root = keep.tile([P, width], F32, name="root")
         nc.vector.tensor_scalar(root[:], twice_root[:], 0.5, None, ALU.mult)
 
+        picked_scales = keep.tile([P, S], U8, name="picked_scales", align_bytes=64)
+        nc.vector.tensor_copy(picked_scales[:], tab_scale_sb[:].bitcast(U8).indirect(offs_sb[:]))
         v_scales = keep.tile([P, S], U8, name="v_scales", align_bytes=64)
-        nc.vector.tensor_copy(v_scales[:], tab_scale_sb[:].bitcast(U8).indirect(offs_sb[:]))
+        nc.vector.tensor_copy(v_scales[:].bitcast(I32), picked_scales[:].bitcast(I32))
+        for a, i in [(a, i) for a in range(K_PASSES) for i in range(1, 4)]:
+            src, dst = 4 * a + 8 * i, 4 * a + i
+            nc.scalar.dma_start(v_scales[dst:P:32].bitcast(I32), picked_scales[src:P:32].bitcast(I32))
         v_words = []
         for a in range(K_PASSES):
             picked = keep.tile([P, S], U32, name="v_words%d" % a, align_bytes=64)
@@ -219,7 +223,10 @@ def tile_list_paged_relu2_compact_kernel(
                 if shared and part.start == 0:
                     nc.vector.tensor_tensor(h_by_token[:, part], values, values, ALU.mult)
                 else:
-                    nc.scalar.activation(h_by_token[:, part], values, ACT.Square)
+                    runs = "p (c i) t -> p c t i"
+                    nc.scalar.activation(
+                        h_by_token[:, part].rearrange(runs, i=PACK), values.rearrange(runs, i=PACK), ACT.Square
+                    )
             for part in parts:
                 signs = sign[:, g : g + 1, :].to_broadcast([P, step, PACK])
                 nc.vector.tensor_tensor(h_by_token[:, part], h_by_token[:, part], signs, ALU.mult)

@@ -29,11 +29,8 @@ BANK = 512
 QUADRANTS = 4
 TINY = 1e-30
 
-SCALAR_CASTS = [(0, 0, 0), (0, 0, 1), (0, 1, 1)]
-LAST_PIECE = None
-GORDER = (1, 0, 2)
-SCATTER_RUNS = [(n, c, c + 1) for c in range(2) for n in range(ROW_TILES)]
-SCATTER_RUNS = SCATTER_RUNS + [(0, 2, 3), (1, 2, 3), (0, 3, 4), (1, 3, 4), (2, 2, 4), (3, 2, 4)]
+
+ROUNDED_KIB = {(0, 0): 48, (0, 1): 52, (1, 0): 40, (1, 1): 56, (2, 0): 48, (2, 1): 52}
 
 
 def tile_list_paged_relu2_compact_kernel(
@@ -42,45 +39,40 @@ def tile_list_paged_relu2_compact_kernel(
     nc = tc.nc
     with ExitStack() as ctx:
         keep = ctx.enter_context(tc.tile_pool(name="keep", bufs=1))
-        cast_ring = ctx.enter_context(tc.tile_pool(name="cast_ring", bufs=3))
+        reused = ctx.enter_context(tc.tile_pool(name="reused", bufs=1))
+
+        def placed(shape, dtype, name, kib):
+            return reused.tile(shape, dtype, name=name, offset=kib * 1024, align_bytes=64)
+
         psum_a = ctx.enter_context(tc.psum_pool(name="psum_a", bufs=4))
         psum_y = ctx.enter_context(tc.psum_pool(name="psum_y", bufs=4))
 
+        w1_raw = {}
+
+        def load_w1(g, a, kib):
+            piece = placed([P, PACK, PASS], F32, "w1_raw%d%d" % (g, a), kib)
+            rows = w1[PASS * a : PASS * (a + 1), PASS * g : PASS * (g + 1)]
+            nc.sync.dma_start(piece[:], rows.rearrange("(p j) c -> p j c", j=PACK))
+            w1_raw[g, a] = piece
+
         offs_sb = keep.tile([P, S // LIST_ROWS], U16, name="offs_sb")
         nc.sync.dma_start(offs_sb[:], offs)
-        tab_word_sb = []
-
-        def load_table(a):
-            words = keep.tile([P, T], I32, name="tab_word%d" % a, tag="big%d" % a, align_bytes=64)
-            nc.sync.dma_start(words[:], tab_words[a].rearrange("p t i -> p (t i)").bitcast(I32))
-            tab_word_sb.append(words)
-
         gain_sb = keep.tile([P, GROUPS, PACK], F32, name="gain_sb")
         nc.sync.dma_start(gain_sb[:], gain.rearrange("(g p t) -> p g t", p=P, t=PACK))
         offs2_sb = keep.tile([P, S // LIST_ROWS], U16, name="offs2_sb")
         nc.sync.dma_start(offs2_sb[:], offs2)
-
+        load_w1(0, 0, 0)
         tab_scale_sb = keep.tile([P, T // 4], I32, name="tab_scale_sb", align_bytes=64)
         nc.vector.memset(tab_scale_sb[:], 0)
         tab_scale_hbm = tab_scales.bitcast(I32)
         for a in range(K_PASSES):
             nc.sync.dma_start(tab_scale_sb[4 * a : P : 8, :], tab_scale_hbm[a])
+        load_w1(0, 1, 8)
+        tab_word_sb = []
         for a in range(K_PASSES):
-            load_table(a)
-
-        w1_raw = {}
-
-        def load_w1(g, a, dst):
-            rows = w1[PASS * a : PASS * (a + 1), PASS * g : PASS * (g + 1)]
-            src = rows.rearrange("(p j) c -> p j c", j=PACK)
-            step = PASS // 2 if (g, a) == LAST_PIECE else PASS
-            for first in range(0, PASS, step):
-                nc.sync.dma_start(dst[:, :, first : first + step], src[:, :, first : first + step])
-            w1_raw[g, a] = dst
-
-        for a in range(K_PASSES):
-            piece = keep.tile([P, PACK, PASS], F32, name="w1_raw0%d" % a, tag="first%d" % a, align_bytes=64)
-            load_w1(0, a, piece[:])
+            words = placed([P, T], I32, "tab_word%d" % a, 16 + 16 * a)
+            nc.sync.dma_start(words[:], tab_words[a].rearrange("p t i -> p (t i)").bitcast(I32))
+            tab_word_sb.append(words)
 
         gain_flat = gain_sb[:].rearrange("p g t -> p (g t)")
         width = GROUPS * PACK
@@ -107,16 +99,6 @@ def tile_list_paged_relu2_compact_kernel(
 
         picked_scales = keep.tile([P, S], U8, name="picked_scales", align_bytes=64)
         nc.vector.tensor_copy(picked_scales[:], tab_scale_sb[:].bitcast(U8).indirect(offs_sb[:]))
-        v_scales = keep.tile([P, S], U8, name="v_scales", align_bytes=64)
-        nc.vector.tensor_copy(v_scales[:].bitcast(I32), picked_scales[:].bitcast(I32))
-        for a, i in [(a, i) for a in range(K_PASSES) for i in range(1, 4)]:
-            src, dst = 4 * a + 8 * i, 4 * a + i
-            nc.scalar.dma_start(v_scales[dst:P:32].bitcast(I32), picked_scales[src:P:32].bitcast(I32))
-        v_words = []
-        for a in range(K_PASSES):
-            picked = keep.tile([P, S], U32, name="v_words%d" % a, align_bytes=64)
-            nc.vector.tensor_copy(picked[:], tab_word_sb[a][:].bitcast(U32).indirect(offs_sb[:]))
-            v_words.append(picked)
 
         slots = []
         for n in range(ROW_TILES):
@@ -124,71 +106,57 @@ def tile_list_paged_relu2_compact_kernel(
             nc.vector.memset(rows_out[:], 0.0)
             slots.append(rows_out)
 
-        for g in range(1, GROUPS):
-            pieces = keep.tile(
-                [P, K_PASSES, PACK, PASS], F32, name="w1_raw%d" % g, tag="big%d" % (g - 1), align_bytes=64
-            )
-            for a in range(K_PASSES):
-                load_w1(g, a, pieces[:, a])
+        v_words = {}
 
-        w1_words, w1_scales = {}, {}
+        def gather_words(a, first, count):
+            picked = keep.tile([P, CHUNK * count], U32, name="v_words%d%d" % (a, first), align_bytes=64)
+            entries = offs_sb[:, CHUNK // LIST_ROWS * first : CHUNK // LIST_ROWS * (first + count)]
+            nc.vector.tensor_copy(picked[:], tab_word_sb[a][:].bitcast(U32).indirect(entries))
+            for c in range(count):
+                v_words[a, first + c] = (picked, c)
 
-        def quantise_w1(g, a):
-            if g == 0:
-                rounded = keep.tile([P, PACK * PASS], BF16, name="r0%d" % a, tag="r0%d" % a, align_bytes=64)
+        w1_rounded, w1_words, w1_scales = {}, {}, {}
+
+        def round_w1(g, a, half, engine):
+            if half == 0:
+                w1_rounded[g, a] = placed([P, PACK * PASS], BF16, "r%d%d" % (g, a), ROUNDED_KIB[g, a])
+            dst = w1_rounded[g, a][:].rearrange("p (t m j) -> p m j t", t=PACK, j=PACK)
+            src = w1_raw[g, a][:].rearrange("p j (m t) -> p m j t", t=PACK)
+            pair = slice(2 * half, 2 * half + 2)
+            if engine == "scalar":
+                nc.scalar.copy(dst[:, :, :, pair], src[:, :, :, pair])
             else:
-                rounded = cast_ring.tile([P, PACK * PASS], BF16, name="rounded", align_bytes=64)
-            dst = rounded[:].rearrange("p (t m j) -> p m j t", t=PACK, j=PACK)
-            src = w1_raw[g, a].rearrange("p j (m t) -> p m j t", t=PACK)
+                nc.vector.tensor_copy(dst[:, :, :, pair], src[:, :, :, pair])
+
+        def quantise_w1(g, a, half):
+            if half == 0:
+                w1_words[g, a] = keep.tile([P, PASS], U32, name="w1_words%d%d" % (g, a), align_bytes=64)
+                w1_scales[g, a] = keep.tile([P, PASS], U8, name="w1_scales%d%d" % (g, a), align_bytes=64)
+            cols = slice(PASS // 2 * half, PASS // 2 * (half + 1))
+            nc.vector.quantize_mx(
+                out=w1_words[g, a][:, cols].bitcast(FP8X4),
+                scales=w1_scales[g, a][:, cols],
+                in_=w1_rounded[g, a][:, PACK * cols.start : PACK * cols.stop],
+            )
+
+        def prepare_w1(g, a, engine):
             for half in range(2):
-                if (g, a) == LAST_PIECE:
-                    rows = slice(P // 2 * half, P // 2 * (half + 1))
-                    nc.vector.tensor_copy(dst[:, rows], src[:, rows])
-                    continue
-                pair = slice(2 * half, 2 * half + 2)
-                if (g, a, half) in SCALAR_CASTS:
-                    nc.scalar.copy(dst[:, :, :, pair], src[:, :, :, pair])
-                else:
-                    nc.vector.tensor_copy(dst[:, :, :, pair], src[:, :, :, pair])
-            codes = keep.tile([P, PASS], U32, name="w1_words%d%d" % (g, a), align_bytes=64)
-            scales = keep.tile([P, PASS], U8, name="w1_scales%d%d" % (g, a), align_bytes=64)
+                round_w1(g, a, half, engine)
             for half in range(2):
-                cols = slice(PASS // 2 * half, PASS // 2 * (half + 1))
-                nc.vector.quantize_mx(
-                    out=codes[:, cols].bitcast(FP8X4),
-                    scales=scales[:, cols],
-                    in_=rounded[:, PACK * cols.start : PACK * cols.stop],
-                )
-            w1_words[g, a], w1_scales[g, a] = codes, scales
+                quantise_w1(g, a, half)
 
-        quantise_w1(0, 0)
-        w2_scale_sb = keep.tile([P, GROUPS, N], U8, name="w2_scale_sb", tag="r00", align_bytes=64)
-        nc.vector.memset(w2_scale_sb[:].bitcast(I32), 0)
-        quantise_w1(0, 1)
-
-        w2_word_sb = keep.tile([P, GROUPS, 2 * N], U8, name="w2_word_sb", tag="first0", align_bytes=64)
-        nc.sync.dma_start(w2_word_sb[:].bitcast(I32), w2_words.bitcast(I32).rearrange("g p c -> p g c"))
-        w2_scale_hbm = w2_scales.bitcast(I32).rearrange("g q c -> q g c")
-        for q in range(QUADRANTS):
-            nc.sync.dma_start(w2_scale_sb[32 * q : 32 * q + 4].bitcast(I32), w2_scale_hbm[4 * q : 4 * q + 4])
-        b2_sb = keep.tile([P, ROW_TILES], F32, name="b2_sb", tag="r01", align_bytes=64)
-        with nc.allow_non_contiguous_dma(reason="one bias value for each partition and row tile"):
-            nc.sync.dma_start(b2_sb[:], b2.rearrange("(n p) -> p n", p=P))
-        wgo_sb = keep.tile([P, S], F32, name="wgo_sb", tag="first1", align_bytes=64)
-        nc.sync.dma_start(wgo_sb[:], wgo)
-
-        h_words, h_scales, rectified, y_acc = {}, {}, {}, {}
+        h_tiles, h_words, h_scales, rectified, y_acc = {}, {}, {}, {}, {}
         y_sb = [keep.tile([P, S], F32, name="y%d" % n) for n in range(ROW_TILES)]
 
         def rectify(g, first, count, vector_banks=()):
             width = CHUNK * count
             tokens = slice(CHUNK * first, CHUNK * first + width)
             per_bank = BANK // width
-            tag = "unit%d%d" % (first, g)
-            values = keep.tile([P, PACK, width], F32, name="values%d%d" % (first, g), tag=tag, align_bytes=64)
+            values = keep.tile([P, PACK, width], F32, name="values%d%d" % (first, g), tag="v%d%d" % (first, g), align_bytes=64)
             for bank in range(PACK // per_bank):
                 acc = psum_a.tile([P, per_bank, width], F32, name="acc")
                 for a in range(K_PASSES):
+                    picked, c = v_words[a, first]
                     for u in range(per_bank):
                         t = per_bank * bank + u
                         cols = slice(P * t, P * (t + 1))
@@ -196,7 +164,7 @@ def tile_list_paged_relu2_compact_kernel(
                             out=acc[:, u, :],
                             lhsT=w1_words[g, a][:, cols].bitcast(FP8X4),
                             lhsT_scale=w1_scales[g, a][:, cols],
-                            rhs=v_words[a][:, tokens].bitcast(FP8X4),
+                            rhs=picked[:, CHUNK * c : CHUNK * c + width].bitcast(FP8X4),
                             rhs_scale=v_scales[4 * a :, tokens],
                             start=(a == 0 and u == 0),
                             stop=(a == K_PASSES - 1 and u == per_bank - 1),
@@ -211,41 +179,45 @@ def tile_list_paged_relu2_compact_kernel(
             for c in range(count):
                 rectified[first + c, g] = values[:, :, CHUNK * c : CHUNK * (c + 1)]
 
-        def quantise(g, c, step=CHUNK, shared=False):
-            tag = "h%d%d" % (c % 2, g)
-            h = keep.tile([P, CHUNK * PACK], BF16, name="h%d%d" % (c, g), tag=tag, align_bytes=64)
-            codes = keep.tile([P, CHUNK], U32, name="h_words%d%d" % (c, g), align_bytes=64)
-            scales = keep.tile([P, CHUNK], U8, name="h_scales%d%d" % (c, g), align_bytes=64)
-            parts = [slice(x, x + step) for x in range(0, CHUNK, step)]
-            h_by_token = h[:].rearrange("p (c t) -> p c t", t=PACK)
-            for part in parts:
-                values = rectified[c, g][:, :, part].rearrange("p t c -> p c t")
-                if shared and part.start == 0:
-                    nc.vector.tensor_tensor(h_by_token[:, part], values, values, ALU.mult)
-                else:
-                    runs = "p (c i) t -> p c t i"
-                    nc.scalar.activation(
-                        h_by_token[:, part].rearrange(runs, i=PACK), values.rearrange(runs, i=PACK), ACT.Square
-                    )
-            for part in parts:
-                signs = sign[:, g : g + 1, :].to_broadcast([P, step, PACK])
-                nc.vector.tensor_tensor(h_by_token[:, part], h_by_token[:, part], signs, ALU.mult)
-            for part in parts:
-                nc.vector.quantize_mx(
-                    out=codes[:, part].bitcast(FP8X4),
-                    scales=scales[:, part],
-                    in_=h[:, PACK * part.start : PACK * part.stop],
+        def square(g, c, part=slice(0, CHUNK), tag=None):
+            if part.start == 0:
+                h_tiles[c, g] = keep.tile(
+                    [P, CHUNK * PACK], BF16, name="h%d%d" % (c, g), tag=tag or "h%d%d" % (c, g), align_bytes=64
                 )
-            h_words[c, g], h_scales[c, g] = codes, scales
+            runs = "p (c i) t -> p c t i"
+            dst = h_tiles[c, g][:].rearrange("p (c t) -> p c t", t=PACK)[:, part]
+            src = rectified[c, g][:, :, part].rearrange("p t c -> p c t")
+            nc.scalar.activation(dst.rearrange(runs, i=PACK), src.rearrange(runs, i=PACK), ACT.Square)
 
-        def project(c):
+        def apply_sign(g, c, part=slice(0, CHUNK), kib=None):
+            src = h_tiles[c, g][:].rearrange("p (c t) -> p c t", t=PACK)[:, part]
+            if kib is not None:
+                h_tiles[c, g] = placed([P, CHUNK * PACK], BF16, "signed%d%d" % (c, g), kib)
+            dst = h_tiles[c, g][:].rearrange("p (c t) -> p c t", t=PACK)[:, part]
+            signs = sign[:, g : g + 1, :].to_broadcast([P, part.stop - part.start, PACK])
+            nc.vector.tensor_tensor(dst, src, signs, ALU.mult)
+
+        def quantise_h(g, c, part=slice(0, CHUNK)):
+            if part.start == 0:
+                h_words[c, g] = keep.tile([P, CHUNK], U32, name="h_words%d%d" % (c, g), align_bytes=64)
+                h_scales[c, g] = keep.tile([P, CHUNK], U8, name="h_scales%d%d" % (c, g), align_bytes=64)
+            nc.vector.quantize_mx(
+                out=h_words[c, g][:, part].bitcast(FP8X4),
+                scales=h_scales[c, g][:, part],
+                in_=h_tiles[c, g][:, PACK * part.start : PACK * part.stop],
+            )
+
+        def project(c, order, groups):
             for n in range(ROW_TILES):
-                acc = psum_y.tile([P, CHUNK], F32, name="y_acc")
-                passes = [(g, first) for g in (GORDER if c == 0 else range(GROUPS)) for first in range(0, CHUNK, P)]
+                if groups[0] == order[0]:
+                    y_acc[c, n] = psum_y.tile([P, CHUNK], F32, name="y_acc")
+                passes = [(g, first) for g in order for first in range(0, CHUNK, P)]
                 for g, first in passes:
+                    if g not in groups:
+                        continue
                     part = slice(first, first + P)
                     nc.tensor.matmul_mx(
-                        out=acc[:, part],
+                        out=y_acc[c, n][:, part],
                         lhsT=w2_word_sb[:, g, 2 * P * n : 2 * P * (n + 1)].bitcast(FP4X4),
                         lhsT_scale=w2_scale_sb[:, g, P * n : P * (n + 1)],
                         rhs=h_words[c, g][:, part].bitcast(FP8X4),
@@ -253,61 +225,122 @@ def tile_list_paged_relu2_compact_kernel(
                         start=((g, first) == passes[0]),
                         stop=((g, first) == passes[-1]),
                     )
-                y_acc[c, n] = acc
 
         def add_bias(c, n):
             dst = y_sb[n][:, CHUNK * c : CHUNK * (c + 1)]
             nc.scalar.activation(dst, y_acc[c, n][:], ACT.Identity, bias=b2_sb[:, n : n + 1])
 
-        quantise_w1(1, 0)
-        quantise_w1(1, 1)
-        rectify(0, 0, 2)
-        quantise(0, 0)
-        quantise_w1(2, 0)
-        quantise_w1(2, 1)
-        quantise(0, 1)
-        rectify(1, 0, 2)
-        quantise(1, 0)
-        rectify(2, 0, 1)
-        quantise(2, 0, step=P, shared=True)
-        quantise(1, 1)
-        project(0)
-        add_bias(0, 0)
-        add_bias(0, 1)
-        rectify(2, 1, 1)
-        rectify(0, 2, 2)
-        quantise(2, 1)
-        add_bias(0, 2)
-        project(1)
-        add_bias(0, 3)
-        rectify(1, 2, 1)
-        rectify(2, 2, 1)
-        quantise(0, 2)
-        add_bias(1, 0)
-        quantise(1, 2)
-        add_bias(1, 1)
-        rectify(1, 3, 1)
-        quantise(2, 2)
-        add_bias(1, 2)
-        project(2)
-        add_bias(1, 3)
-        quantise(0, 3)
-        rectify(2, 3, 1)
-        quantise(1, 3)
-        add_bias(2, 2)
-        add_bias(2, 3)
-        quantise(2, 3)
-        add_bias(2, 0)
-        add_bias(2, 1)
-        project(3)
-        add_bias(3, 0)
-        add_bias(3, 1)
-        add_bias(3, 2)
-        add_bias(3, 3)
-
-        for n, first, last in SCATTER_RUNS:
+        def scatter(n, first, last):
             places = offs2_sb[:, CHUNK // LIST_ROWS * first : CHUNK // LIST_ROWS * last]
             tokens = slice(CHUNK * first, CHUNK * last)
             nc.vector.tensor_tensor(slots[n][:].indirect(places), y_sb[n][:, tokens], wgo_sb[:, tokens], ALU.mult)
             if last == CHUNKS:
                 nc.sync.dma_start(out[P * n : P * (n + 1), :], slots[n][:])
+
+        halves = [slice(0, P), slice(P, CHUNK)]
+        up, down = (0, 1, 2), (2, 1, 0)
+        prepare_w1(0, 0, "scalar")
+        for half in range(2):
+            round_w1(0, 1, half, "scalar")
+        v_scales = placed([P, S], U8, "v_scales", 8)
+        nc.vector.tensor_copy(v_scales[:].bitcast(I32), picked_scales[:].bitcast(I32))
+        for a, i in [(a, i) for a in range(K_PASSES) for i in range(1, 4)]:
+            src, dst = 4 * a + 8 * i, 4 * a + i
+            nc.scalar.dma_start(v_scales[dst:P:32].bitcast(I32), picked_scales[src:P:32].bitcast(I32))
+
+        gather_words(0, 0, 4)
+        for half in range(2):
+            quantise_w1(0, 1, half)
+        load_w1(1, 0, 16)
+        load_w1(1, 1, 24)
+        gather_words(1, 0, 2)
+        gather_words(1, 2, 2)
+        load_w1(2, 0, 32)
+        prepare_w1(1, 0, "vector")
+        load_w1(2, 1, 40)
+        prepare_w1(1, 1, "vector")
+        w2_word_sb = placed([P, GROUPS, 2 * N], U8, "w2_word_sb", 24)
+        nc.sync.dma_start(w2_word_sb[:].bitcast(I32), w2_words.bitcast(I32).rearrange("g p c -> p g c"))
+        wgo_sb = placed([P, S], F32, "wgo_sb", 27)
+        nc.sync.dma_start(wgo_sb[:], wgo)
+        b2_sb = placed([P, ROW_TILES], F32, "b2_sb", 31)
+        with nc.allow_non_contiguous_dma(reason="one bias value for each partition and row tile"):
+            nc.sync.dma_start(b2_sb[:], b2.rearrange("(n p) -> p n", p=P))
+        w2_scale_sb = placed([P, GROUPS, N], U8, "w2_scale_sb", 56)
+        nc.vector.memset(w2_scale_sb[:].bitcast(I32), 0)
+        w2_scale_hbm = w2_scales.bitcast(I32).rearrange("g q c -> q g c")
+        for q in range(QUADRANTS):
+            nc.sync.dma_start(w2_scale_sb[32 * q : 32 * q + 4].bitcast(I32), w2_scale_hbm[4 * q : 4 * q + 4])
+        rectify(0, 0, 2)
+        square(0, 0)
+        square(0, 1)
+        prepare_w1(2, 0, "vector")
+        prepare_w1(2, 1, "vector")
+
+        def finish(g, c, parts=(slice(0, CHUNK),)):
+            for part in parts:
+                apply_sign(g, c, part)
+            for part in parts:
+                quantise_h(g, c, part)
+
+        rectify(1, 0, 2)
+        square(1, 0)
+        square(1, 1)
+        rectify(2, 0, 1)
+        for part in halves:
+            square(2, 0, part)
+        apply_sign(0, 0, kib=40)
+        apply_sign(1, 0, kib=42)
+        quantise_h(0, 0)
+        quantise_h(1, 0)
+        project(0, up, (0, 1))
+        finish(2, 0, halves)
+        project(0, up, (2,))
+        add_bias(0, 0)
+        rectify(2, 1, 1)
+        rectify(0, 2, 1)
+        apply_sign(0, 1, kib=44)
+        apply_sign(1, 1, kib=46)
+        quantise_h(0, 1)
+        quantise_h(1, 1)
+        add_bias(0, 1)
+        square(2, 1)
+        finish(2, 1, halves)
+        add_bias(0, 2)
+        add_bias(0, 3)
+        rectify(1, 2, 1)
+        square(0, 2)
+        project(1, down, down)
+        finish(0, 2)
+        rectify(2, 2, 1)
+        add_bias(1, 0)
+        square(1, 2)
+        finish(1, 2)
+        add_bias(1, 1)
+        square(2, 2)
+        finish(2, 2, halves)
+        rectify(0, 3, 1)
+        add_bias(1, 2)
+        rectify(1, 3, 1)
+        add_bias(1, 3)
+        square(0, 3)
+        finish(0, 3)
+        rectify(2, 3, 1)
+        project(2, down, down)
+        square(1, 3)
+        finish(1, 3)
+        square(2, 3)
+        finish(2, 3, halves)
+        for n in range(ROW_TILES):
+            add_bias(2, n)
+        project(3, down, down)
+        for n in range(ROW_TILES):
+            add_bias(3, n)
+        for c in range(2):
+            for n in range(ROW_TILES):
+                scatter(n, c, c + 1)
+        for c in range(2, CHUNKS):
+            for n in range(2):
+                scatter(n, c, c + 1)
+        scatter(2, 2, 4)
+        scatter(3, 2, 4)

@@ -30,7 +30,10 @@ QUADRANTS = 4
 TINY = 1e-30
 
 
-ROUNDED_KIB = {(0, 0): 48, (0, 1): 52, (1, 0): 40, (1, 1): 56, (2, 0): 48, (2, 1): 52}
+VECTOR_TOKENS = 160
+A_BANKS = {(0, 0): 0, (1, 0): 4, (2, 0): 0, (2, 1): 2, (0, 2): 0, (1, 2): 4, (2, 2): 6, (0, 3): 4, (1, 3): 6, (2, 3): 4}
+Y_BANKS = [(4, 5, 6, 7), (2, 3, 0, 1), (2, 3, 0, 1), (6, 7, 4, 5)]
+ROUNDED_KIB = {(0, 0): 56, (0, 1): 60, (1, 0): 48, (1, 1): 64, (2, 0): 56, (2, 1): 60}
 
 
 def tile_list_paged_relu2_compact_kernel(
@@ -42,10 +45,9 @@ def tile_list_paged_relu2_compact_kernel(
         reused = ctx.enter_context(tc.tile_pool(name="reused", bufs=1))
 
         def placed(shape, dtype, name, kib):
-            return reused.tile(shape, dtype, name=name, offset=kib * 1024, align_bytes=64)
+            return reused.tile(shape, dtype, name=name, offset=int(kib * 1024), align_bytes=64)
 
-        psum_a = ctx.enter_context(tc.psum_pool(name="psum_a", bufs=4))
-        psum_y = ctx.enter_context(tc.psum_pool(name="psum_y", bufs=4))
+        psum = ctx.enter_context(tc.psum_pool(name="psum", bufs=1))
 
         w1_raw = {}
 
@@ -70,7 +72,7 @@ def tile_list_paged_relu2_compact_kernel(
         load_w1(0, 1, 8)
         tab_word_sb = []
         for a in range(K_PASSES):
-            words = placed([P, T], I32, "tab_word%d" % a, 16 + 16 * a)
+            words = placed([P, T], I32, "tab_word%d" % a, 20 + 20 * a)
             nc.sync.dma_start(words[:], tab_words[a].rearrange("p t i -> p (t i)").bitcast(I32))
             tab_word_sb.append(words)
 
@@ -101,7 +103,7 @@ def tile_list_paged_relu2_compact_kernel(
         nc.vector.tensor_copy(picked_scales[:], tab_scale_sb[:].bitcast(U8).indirect(offs_sb[:]))
 
         slots = []
-        for n in range(ROW_TILES):
+        for n in range(ROW_TILES - 1):
             rows_out = keep.tile([P, T2], F32, name="slots%d" % n)
             nc.vector.memset(rows_out[:], 0.0)
             slots.append(rows_out)
@@ -145,16 +147,20 @@ def tile_list_paged_relu2_compact_kernel(
             for half in range(2):
                 quantise_w1(g, a, half)
 
-        h_tiles, h_words, h_scales, rectified, y_acc = {}, {}, {}, {}, {}
+        h_tiles, signed, h_words, h_scales, rectified, y_acc, y_parts = {}, {}, {}, {}, {}, {}, {}
         y_sb = [keep.tile([P, S], F32, name="y%d" % n) for n in range(ROW_TILES)]
 
-        def rectify(g, first, count, vector_banks=()):
+        def rectify(g, first, count, vector_banks=(), kib=None):
             width = CHUNK * count
             tokens = slice(CHUNK * first, CHUNK * first + width)
             per_bank = BANK // width
-            values = keep.tile([P, PACK, width], F32, name="values%d%d" % (first, g), tag="v%d%d" % (first, g), align_bytes=64)
+            if kib is None:
+                values = keep.tile([P, PACK, width], F32, name="values%d%d" % (first, g), align_bytes=64)
+            else:
+                values = placed([P, PACK, width], F32, "values%d%d" % (first, g), kib)
             for bank in range(PACK // per_bank):
-                acc = psum_a.tile([P, per_bank, width], F32, name="acc")
+                where = (A_BANKS[g, first] + bank) * BANK * 4
+                acc = psum.tile([P, per_bank, width], F32, name="a%d%d%d" % (g, first, bank), offset=where)
                 for a in range(K_PASSES):
                     picked, c = v_words[a, first]
                     for u in range(per_bank):
@@ -179,38 +185,45 @@ def tile_list_paged_relu2_compact_kernel(
             for c in range(count):
                 rectified[first + c, g] = values[:, :, CHUNK * c : CHUNK * (c + 1)]
 
-        def square(g, c, part=slice(0, CHUNK), tag=None):
-            if part.start == 0:
-                h_tiles[c, g] = keep.tile(
-                    [P, CHUNK * PACK], BF16, name="h%d%d" % (c, g), tag=tag or "h%d%d" % (c, g), align_bytes=64
-                )
+        def square(g, c, part=slice(0, CHUNK), engine="scalar", kib=None):
+            if kib is not None:
+                h_tiles[c, g] = placed([P, CHUNK * PACK], BF16, "h%d%d" % (c, g), kib)
+            elif (c, g) not in h_tiles:
+                h_tiles[c, g] = keep.tile([P, CHUNK * PACK], BF16, name="h%d%d" % (c, g), align_bytes=64)
             runs = "p (c i) t -> p c t i"
             dst = h_tiles[c, g][:].rearrange("p (c t) -> p c t", t=PACK)[:, part]
             src = rectified[c, g][:, :, part].rearrange("p t c -> p c t")
-            nc.scalar.activation(dst.rearrange(runs, i=PACK), src.rearrange(runs, i=PACK), ACT.Square)
+            dst, src = dst.rearrange(runs, i=PACK), src.rearrange(runs, i=PACK)
+            if engine == "scalar":
+                nc.scalar.activation(dst, src, ACT.Square)
+            else:
+                nc.vector.tensor_tensor(dst, src, src, ALU.mult)
 
         def apply_sign(g, c, part=slice(0, CHUNK), kib=None):
             src = h_tiles[c, g][:].rearrange("p (c t) -> p c t", t=PACK)[:, part]
             if kib is not None:
-                h_tiles[c, g] = placed([P, CHUNK * PACK], BF16, "signed%d%d" % (c, g), kib)
-            dst = h_tiles[c, g][:].rearrange("p (c t) -> p c t", t=PACK)[:, part]
+                signed[c, g] = placed([P, CHUNK * PACK], BF16, "signed%d%d" % (c, g), kib)
+            dst = signed.setdefault((c, g), h_tiles[c, g])[:].rearrange("p (c t) -> p c t", t=PACK)[:, part]
             signs = sign[:, g : g + 1, :].to_broadcast([P, part.stop - part.start, PACK])
             nc.vector.tensor_tensor(dst, src, signs, ALU.mult)
 
-        def quantise_h(g, c, part=slice(0, CHUNK)):
+        def quantise_h(g, c, part=slice(0, CHUNK), kib=None):
             if part.start == 0:
-                h_words[c, g] = keep.tile([P, CHUNK], U32, name="h_words%d%d" % (c, g), align_bytes=64)
+                if kib is None:
+                    h_words[c, g] = keep.tile([P, CHUNK], U32, name="h_words%d%d" % (c, g), align_bytes=64)
+                else:
+                    h_words[c, g] = placed([P, CHUNK], U32, "h_words%d%d" % (c, g), kib)
                 h_scales[c, g] = keep.tile([P, CHUNK], U8, name="h_scales%d%d" % (c, g), align_bytes=64)
             nc.vector.quantize_mx(
                 out=h_words[c, g][:, part].bitcast(FP8X4),
                 scales=h_scales[c, g][:, part],
-                in_=h_tiles[c, g][:, PACK * part.start : PACK * part.stop],
+                in_=signed[c, g][:, PACK * part.start : PACK * part.stop],
             )
 
         def project(c, order, groups):
             for n in range(ROW_TILES):
                 if groups[0] == order[0]:
-                    y_acc[c, n] = psum_y.tile([P, CHUNK], F32, name="y_acc")
+                    y_acc[c, n] = psum.tile([P, CHUNK], F32, name="y%d%d" % (c, n), offset=Y_BANKS[c][n] * BANK * 4)
                 passes = [(g, first) for g in order for first in range(0, CHUNK, P)]
                 for g, first in passes:
                     if g not in groups:
@@ -226,14 +239,17 @@ def tile_list_paged_relu2_compact_kernel(
                         stop=((g, first) == passes[-1]),
                     )
 
-        def add_bias(c, n):
+        def add_bias(c, n, kib=None):
             dst = y_sb[n][:, CHUNK * c : CHUNK * (c + 1)]
+            if kib is not None:
+                dst = placed([P, CHUNK], F32, "y_late", kib)[:]
+                y_parts[n, c] = dst
             nc.scalar.activation(dst, y_acc[c, n][:], ACT.Identity, bias=b2_sb[:, n : n + 1])
 
         def scatter(n, first, last):
             places = offs2_sb[:, CHUNK // LIST_ROWS * first : CHUNK // LIST_ROWS * last]
             tokens = slice(CHUNK * first, CHUNK * last)
-            nc.vector.tensor_tensor(slots[n][:].indirect(places), y_sb[n][:, tokens], wgo_sb[:, tokens], ALU.mult)
+            nc.vector.tensor_tensor(slots[n][:].indirect(places), y_parts.get((n, first), y_sb[n][:, tokens]), wgo_sb[:, tokens], ALU.mult)
             if last == CHUNKS:
                 nc.sync.dma_start(out[P * n : P * (n + 1), :], slots[n][:])
 
@@ -252,21 +268,23 @@ def tile_list_paged_relu2_compact_kernel(
         for half in range(2):
             quantise_w1(0, 1, half)
         load_w1(1, 0, 16)
-        load_w1(1, 1, 24)
+        slots.append(placed([P, T2], F32, "slots3", 24))
+        nc.vector.memset(slots[3][:], 0.0)
+        load_w1(1, 1, 32)
         gather_words(1, 0, 2)
         gather_words(1, 2, 2)
-        load_w1(2, 0, 32)
+        load_w1(2, 0, 40)
         prepare_w1(1, 0, "vector")
-        load_w1(2, 1, 40)
+        load_w1(2, 1, 48)
         prepare_w1(1, 1, "vector")
-        w2_word_sb = placed([P, GROUPS, 2 * N], U8, "w2_word_sb", 24)
+        w2_word_sb = placed([P, GROUPS, 2 * N], U8, "w2_word_sb", 32)
         nc.sync.dma_start(w2_word_sb[:].bitcast(I32), w2_words.bitcast(I32).rearrange("g p c -> p g c"))
-        wgo_sb = placed([P, S], F32, "wgo_sb", 27)
+        wgo_sb = placed([P, S], F32, "wgo_sb", 35)
         nc.sync.dma_start(wgo_sb[:], wgo)
-        b2_sb = placed([P, ROW_TILES], F32, "b2_sb", 31)
+        b2_sb = placed([P, ROW_TILES], F32, "b2_sb", 39)
         with nc.allow_non_contiguous_dma(reason="one bias value for each partition and row tile"):
             nc.sync.dma_start(b2_sb[:], b2.rearrange("(n p) -> p n", p=P))
-        w2_scale_sb = placed([P, GROUPS, N], U8, "w2_scale_sb", 56)
+        w2_scale_sb = placed([P, GROUPS, N], U8, "w2_scale_sb", 64)
         nc.vector.memset(w2_scale_sb[:].bitcast(I32), 0)
         w2_scale_hbm = w2_scales.bitcast(I32).rearrange("g q c -> q g c")
         for q in range(QUADRANTS):
@@ -285,62 +303,72 @@ def tile_list_paged_relu2_compact_kernel(
 
         rectify(1, 0, 2)
         square(1, 0)
-        square(1, 1)
         rectify(2, 0, 1)
-        for part in halves:
-            square(2, 0, part)
-        apply_sign(0, 0, kib=40)
-        apply_sign(1, 0, kib=42)
+        square(2, 0, halves[0], "vector", kib=10)
+        square(2, 0, slice(P, VECTOR_TOKENS), "vector")
+        square(2, 0, slice(VECTOR_TOKENS, CHUNK))
+        apply_sign(0, 0, kib=48)
+        apply_sign(1, 0, kib=50)
         quantise_h(0, 0)
         quantise_h(1, 0)
         project(0, up, (0, 1))
-        finish(2, 0, halves)
+        for part in halves:
+            apply_sign(2, 0, part)
+        for part in halves:
+            quantise_h(2, 0, part, kib=4)
         project(0, up, (2,))
         add_bias(0, 0)
-        rectify(2, 1, 1)
-        rectify(0, 2, 1)
-        apply_sign(0, 1, kib=44)
-        apply_sign(1, 1, kib=46)
-        quantise_h(0, 1)
-        quantise_h(1, 1)
         add_bias(0, 1)
-        square(2, 1)
-        finish(2, 1, halves)
+        rectify(2, 1, 1)
+        apply_sign(0, 1, halves[0], kib=10)
+        apply_sign(0, 1, halves[1])
+        for part in halves:
+            quantise_h(0, 1, part)
+        square(1, 1, kib=2.5)
+        finish(1, 1, halves)
+        square(2, 1, kib=4.5)
+        finish(2, 1)
         add_bias(0, 2)
+        rectify(0, 2, 1)
         add_bias(0, 3)
         rectify(1, 2, 1)
         square(0, 2)
-        project(1, down, down)
-        finish(0, 2)
+        finish(0, 2, halves)
         rectify(2, 2, 1)
+        project(1, down, down)
         add_bias(1, 0)
         square(1, 2)
         finish(1, 2)
         add_bias(1, 1)
-        square(2, 2)
-        finish(2, 2, halves)
         rectify(0, 3, 1)
+        square(2, 2)
+        finish(2, 2)
         add_bias(1, 2)
-        rectify(1, 3, 1)
         add_bias(1, 3)
+        rectify(1, 3, 1)
         square(0, 3)
-        finish(0, 3)
+        finish(0, 3, halves)
         rectify(2, 3, 1)
         project(2, down, down)
+        add_bias(2, 0)
         square(1, 3)
         finish(1, 3)
-        square(2, 3)
-        finish(2, 3, halves)
-        for n in range(ROW_TILES):
-            add_bias(2, n)
-        project(3, down, down)
+        add_bias(2, 1)
+        square(2, 3, kib=0)
+        apply_sign(2, 3, halves[0], kib=2)
+        apply_sign(2, 3, halves[1])
+        for part in halves:
+            quantise_h(2, 3, part)
+        add_bias(2, 3)
+        add_bias(2, 2, kib=0)
+        project(3, up, (0, 1))
+        project(3, up, (2,))
         for n in range(ROW_TILES):
             add_bias(3, n)
         for c in range(2):
             for n in range(ROW_TILES):
                 scatter(n, c, c + 1)
         for c in range(2, CHUNKS):
-            for n in range(2):
+            for n in range(ROW_TILES - 1):
                 scatter(n, c, c + 1)
-        scatter(2, 2, 4)
         scatter(3, 2, 4)

@@ -31,9 +31,20 @@ TINY = 1e-30
 
 
 VECTOR_TOKENS = 160
-A_BANKS = {(0, 0): 0, (1, 0): 4, (2, 0): 0, (2, 1): 2, (0, 2): 0, (1, 2): 4, (2, 2): 6, (0, 3): 4, (1, 3): 6, (2, 3): 4}
-Y_BANKS = [(4, 5, 6, 7), (2, 3, 0, 1), (2, 3, 0, 1), (6, 7, 4, 5)]
-ROUNDED_KIB = {(0, 0): 56, (0, 1): 60, (1, 0): 48, (1, 1): 64, (2, 0): 56, (2, 1): 60}
+A_BANKS = {
+    (0, 0): (0, 1, 2, 3),
+    (1, 0): (4, 5, 6, 7),
+    (2, 0): (0, 1),
+    (2, 1): (2, 3),
+    (0, 2): (0, 1),
+    (1, 2): (4, 5),
+    (2, 2): (6, 1),
+    (0, 3): (4, 5),
+    (1, 3): (6, 1),
+    (2, 3): (0, 2),
+}
+Y_BANKS = [(4, 5, 6, 7), (0, 2, 3, 7), (4, 5, 3, 7), (6, 1, 0, 2)]
+ROUNDED_KIB = {(0, 0): 64, (0, 1): 68, (1, 0): 41, (1, 1): 72, (2, 0): 64, (2, 1): 68}
 
 
 def tile_list_paged_relu2_compact_kernel(
@@ -72,7 +83,7 @@ def tile_list_paged_relu2_compact_kernel(
         load_w1(0, 1, 8)
         tab_word_sb = []
         for a in range(K_PASSES):
-            words = placed([P, T], I32, "tab_word%d" % a, 20 + 20 * a)
+            words = placed([P, T], I32, "tab_word%d" % a, 20 + 24 * a)
             nc.sync.dma_start(words[:], tab_words[a].rearrange("p t i -> p (t i)").bitcast(I32))
             tab_word_sb.append(words)
 
@@ -147,7 +158,7 @@ def tile_list_paged_relu2_compact_kernel(
             for half in range(2):
                 quantise_w1(g, a, half)
 
-        h_tiles, signed, h_words, h_scales, rectified, y_acc, y_parts = {}, {}, {}, {}, {}, {}, {}
+        h_tiles, batches, h_words, h_scales, rectified, y_acc, y_parts = {}, {}, {}, {}, {}, {}, {}
         y_sb = [keep.tile([P, S], F32, name="y%d" % n) for n in range(ROW_TILES)]
 
         def rectify(g, first, count, vector_banks=(), kib=None):
@@ -159,7 +170,7 @@ def tile_list_paged_relu2_compact_kernel(
             else:
                 values = placed([P, PACK, width], F32, "values%d%d" % (first, g), kib)
             for bank in range(PACK // per_bank):
-                where = (A_BANKS[g, first] + bank) * BANK * 4
+                where = A_BANKS[g, first][bank] * BANK * 4
                 acc = psum.tile([P, per_bank, width], F32, name="a%d%d%d" % (g, first, bank), offset=where)
                 for a in range(K_PASSES):
                     picked, c = v_words[a, first]
@@ -185,13 +196,26 @@ def tile_list_paged_relu2_compact_kernel(
             for c in range(count):
                 rectified[first + c, g] = values[:, :, CHUNK * c : CHUNK * (c + 1)]
 
-        def square(g, c, part=slice(0, CHUNK), engine="scalar", kib=None):
-            if kib is not None:
-                h_tiles[c, g] = placed([P, CHUNK * PACK], BF16, "h%d%d" % (c, g), kib)
-            elif (c, g) not in h_tiles:
-                h_tiles[c, g] = keep.tile([P, CHUNK * PACK], BF16, name="h%d%d" % (c, g), align_bytes=64)
+        def batch(c, groups, kib=None, signed_kib=None, words_kib=None):
+            name = "%d%d" % (c, groups[0])
+            shape = [P, len(groups), CHUNK * PACK]
+            if kib is None:
+                h = keep.tile(shape, BF16, name="h" + name, align_bytes=64)
+            else:
+                h = placed(shape, BF16, "h" + name, kib)
+            signed = h if signed_kib is None else placed(shape, BF16, "signed" + name, signed_kib)
+            if words_kib is None:
+                words = keep.tile([P, len(groups), CHUNK], U32, name="h_words" + name, align_bytes=64)
+            else:
+                words = placed([P, len(groups), CHUNK], U32, "h_words" + name, words_kib)
+            scales = keep.tile([P, len(groups), CHUNK], U8, name="h_scales" + name, align_bytes=64)
+            batches[c, groups[0]] = (groups, h, signed, words, scales)
+            for i, g in enumerate(groups):
+                h_tiles[c, g], h_words[c, g], h_scales[c, g] = h[:, i, :], words[:, i, :], scales[:, i, :]
+
+        def square(g, c, part=slice(0, CHUNK), engine="scalar"):
             runs = "p (c i) t -> p c t i"
-            dst = h_tiles[c, g][:].rearrange("p (c t) -> p c t", t=PACK)[:, part]
+            dst = h_tiles[c, g].rearrange("p (c t) -> p c t", t=PACK)[:, part]
             src = rectified[c, g][:, :, part].rearrange("p t c -> p c t")
             dst, src = dst.rearrange(runs, i=PACK), src.rearrange(runs, i=PACK)
             if engine == "scalar":
@@ -199,25 +223,21 @@ def tile_list_paged_relu2_compact_kernel(
             else:
                 nc.vector.tensor_tensor(dst, src, src, ALU.mult)
 
-        def apply_sign(g, c, part=slice(0, CHUNK), kib=None):
-            src = h_tiles[c, g][:].rearrange("p (c t) -> p c t", t=PACK)[:, part]
-            if kib is not None:
-                signed[c, g] = placed([P, CHUNK * PACK], BF16, "signed%d%d" % (c, g), kib)
-            dst = signed.setdefault((c, g), h_tiles[c, g])[:].rearrange("p (c t) -> p c t", t=PACK)[:, part]
-            signs = sign[:, g : g + 1, :].to_broadcast([P, part.stop - part.start, PACK])
+        def apply_sign(g, c, part=slice(0, CHUNK)):
+            groups, h, signed, words, scales = batches[c, g]
+            src = h[:].rearrange("p g (c t) -> p g c t", t=PACK)[:, :, part]
+            dst = signed[:].rearrange("p g (c t) -> p g c t", t=PACK)[:, :, part]
+            signs = sign[:, g : g + len(groups), :].unsqueeze(2)
+            signs = signs.to_broadcast([P, len(groups), part.stop - part.start, PACK])
             nc.vector.tensor_tensor(dst, src, signs, ALU.mult)
 
-        def quantise_h(g, c, part=slice(0, CHUNK), kib=None):
-            if part.start == 0:
-                if kib is None:
-                    h_words[c, g] = keep.tile([P, CHUNK], U32, name="h_words%d%d" % (c, g), align_bytes=64)
-                else:
-                    h_words[c, g] = placed([P, CHUNK], U32, "h_words%d%d" % (c, g), kib)
-                h_scales[c, g] = keep.tile([P, CHUNK], U8, name="h_scales%d%d" % (c, g), align_bytes=64)
+        def quantise_h(g, c, part=slice(0, CHUNK)):
+            groups, h, signed, words, scales = batches[c, g]
+            cols = slice(part.start, part.stop + CHUNK * (len(groups) - 1))
             nc.vector.quantize_mx(
-                out=h_words[c, g][:, part].bitcast(FP8X4),
-                scales=h_scales[c, g][:, part],
-                in_=signed[c, g][:, PACK * part.start : PACK * part.stop],
+                out=words[:].rearrange("p g c -> p (g c)")[:, cols].bitcast(FP8X4),
+                scales=scales[:].rearrange("p g c -> p (g c)")[:, cols],
+                in_=signed[:].rearrange("p g c -> p (g c)")[:, PACK * cols.start : PACK * cols.stop],
             )
 
         def project(c, order, groups):
@@ -273,9 +293,9 @@ def tile_list_paged_relu2_compact_kernel(
         load_w1(1, 1, 32)
         gather_words(1, 0, 2)
         gather_words(1, 2, 2)
-        load_w1(2, 0, 40)
+        load_w1(2, 0, 45)
+        load_w1(2, 1, 53)
         prepare_w1(1, 0, "vector")
-        load_w1(2, 1, 48)
         prepare_w1(1, 1, "vector")
         w2_word_sb = placed([P, GROUPS, 2 * N], U8, "w2_word_sb", 32)
         nc.sync.dma_start(w2_word_sb[:].bitcast(I32), w2_words.bitcast(I32).rearrange("g p c -> p g c"))
@@ -284,91 +304,87 @@ def tile_list_paged_relu2_compact_kernel(
         b2_sb = placed([P, ROW_TILES], F32, "b2_sb", 39)
         with nc.allow_non_contiguous_dma(reason="one bias value for each partition and row tile"):
             nc.sync.dma_start(b2_sb[:], b2.rearrange("(n p) -> p n", p=P))
-        w2_scale_sb = placed([P, GROUPS, N], U8, "w2_scale_sb", 64)
+        w2_scale_sb = placed([P, GROUPS, N], U8, "w2_scale_sb", 72)
         nc.vector.memset(w2_scale_sb[:].bitcast(I32), 0)
         w2_scale_hbm = w2_scales.bitcast(I32).rearrange("g q c -> q g c")
         for q in range(QUADRANTS):
             nc.sync.dma_start(w2_scale_sb[32 * q : 32 * q + 4].bitcast(I32), w2_scale_hbm[4 * q : 4 * q + 4])
+        batch(0, (0, 1), signed_kib=53)
+        batch(0, (2,), kib=10, words_kib=4)
+        batch(1, (0, 1), signed_kib=57)
         rectify(0, 0, 2)
         square(0, 0)
         square(0, 1)
         prepare_w1(2, 0, "vector")
         prepare_w1(2, 1, "vector")
 
-        def finish(g, c, parts=(slice(0, CHUNK),)):
-            for part in parts:
-                apply_sign(g, c, part)
-            for part in parts:
-                quantise_h(g, c, part)
-
         rectify(1, 0, 2)
         square(1, 0)
+        square(1, 1)
         rectify(2, 0, 1)
-        square(2, 0, halves[0], "vector", kib=10)
-        square(2, 0, slice(P, VECTOR_TOKENS), "vector")
-        square(2, 0, slice(VECTOR_TOKENS, CHUNK))
-        apply_sign(0, 0, kib=48)
-        apply_sign(1, 0, kib=50)
+        for part in halves:
+            square(2, 0, part)
+        apply_sign(0, 0)
         quantise_h(0, 0)
-        quantise_h(1, 0)
         project(0, up, (0, 1))
         for part in halves:
             apply_sign(2, 0, part)
         for part in halves:
-            quantise_h(2, 0, part, kib=4)
+            quantise_h(2, 0, part)
         project(0, up, (2,))
         add_bias(0, 0)
         add_bias(0, 1)
+        apply_sign(0, 1)
+        quantise_h(0, 1)
         rectify(2, 1, 1)
-        apply_sign(0, 1, halves[0], kib=10)
-        apply_sign(0, 1, halves[1])
-        for part in halves:
-            quantise_h(0, 1, part)
-        square(1, 1, kib=2.5)
-        finish(1, 1, halves)
-        square(2, 1, kib=4.5)
-        finish(2, 1)
-        add_bias(0, 2)
         rectify(0, 2, 1)
-        add_bias(0, 3)
+        batch(1, (2,), kib=4.5)
+        square(2, 1)
+        apply_sign(2, 1)
+        quantise_h(2, 1)
+        add_bias(0, 2)
         rectify(1, 2, 1)
+        batch(2, (0, 1))
+        batch(2, (2,))
         square(0, 2)
-        finish(0, 2, halves)
+        add_bias(0, 3)
         rectify(2, 2, 1)
         project(1, down, down)
-        add_bias(1, 0)
         square(1, 2)
-        finish(1, 2)
+        apply_sign(0, 2)
+        quantise_h(0, 2)
+        add_bias(1, 0)
         add_bias(1, 1)
-        rectify(0, 3, 1)
         square(2, 2)
-        finish(2, 2)
+        apply_sign(2, 2)
+        quantise_h(2, 2)
         add_bias(1, 2)
-        add_bias(1, 3)
+        rectify(0, 3, 1)
         rectify(1, 3, 1)
+        add_bias(1, 3)
+        batch(3, (0, 1))
+        batch(3, (2,), kib=0, signed_kib=2)
         square(0, 3)
-        finish(0, 3, halves)
         rectify(2, 3, 1)
         project(2, down, down)
-        add_bias(2, 0)
         square(1, 3)
-        finish(1, 3)
-        add_bias(2, 1)
-        square(2, 3, kib=0)
-        apply_sign(2, 3, halves[0], kib=2)
-        apply_sign(2, 3, halves[1])
-        for part in halves:
-            quantise_h(2, 3, part)
+        add_bias(2, 0)
+        square(2, 3)
+        apply_sign(0, 3)
+        apply_sign(2, 3)
+        quantise_h(0, 3)
+        quantise_h(2, 3)
+        add_bias(2, 2)
         add_bias(2, 3)
-        add_bias(2, 2, kib=0)
-        project(3, up, (0, 1))
-        project(3, up, (2,))
+        add_bias(2, 1, kib=0)
+        project(3, up, up)
         for n in range(ROW_TILES):
             add_bias(3, n)
         for c in range(2):
             for n in range(ROW_TILES):
                 scatter(n, c, c + 1)
         for c in range(2, CHUNKS):
-            for n in range(ROW_TILES - 1):
+            for n in range(2):
                 scatter(n, c, c + 1)
+        scatter(2, 2, 4)
         scatter(3, 2, 4)

@@ -350,13 +350,13 @@ def tile_list_paged_relu2_compact_kernel(
         add_bias(0, 3)
         rectify(2, 2, 1)
         project(1, down, down)
-        square(1, 2)
-        apply_sign(0, 2)
-        quantise_h(0, 2)
         add_bias(1, 0)
         add_bias(1, 1)
+        square(1, 2)
         square(2, 2)
+        apply_sign(0, 2)
         apply_sign(2, 2)
+        quantise_h(0, 2)
         quantise_h(2, 2)
         add_bias(1, 2)
         rectify(0, 3, 1)
@@ -365,18 +365,18 @@ def tile_list_paged_relu2_compact_kernel(
         batch(3, (0, 1))
         batch(3, (2,), kib=0, signed_kib=2)
         square(0, 3)
-        rectify(2, 3, 1)
         project(2, down, down)
-        square(1, 3)
         add_bias(2, 0)
+        add_bias(2, 1)
+        rectify(2, 3, 1)
+        square(1, 3)
         square(2, 3)
         apply_sign(0, 3)
         apply_sign(2, 3)
         quantise_h(0, 3)
         quantise_h(2, 3)
-        add_bias(2, 2)
         add_bias(2, 3)
-        add_bias(2, 1, kib=0)
+        add_bias(2, 2, kib=0)
         project(3, up, up)
         for n in range(ROW_TILES):
             add_bias(3, n)
@@ -384,7 +384,6 @@ def tile_list_paged_relu2_compact_kernel(
             for n in range(ROW_TILES):
                 scatter(n, c, c + 1)
         for c in range(2, CHUNKS):
-            for n in range(2):
+            for n in range(ROW_TILES - 1):
                 scatter(n, c, c + 1)
-        scatter(2, 2, 4)
         scatter(3, 2, 4)

@@ -44,7 +44,7 @@ A_BANKS = {
     (2, 3): (0, 2),
 }
 Y_BANKS = [(4, 5, 6, 7), (0, 2, 3, 7), (4, 5, 3, 7), (6, 1, 0, 2)]
-ROUNDED_KIB = {(0, 0): 64, (0, 1): 68, (1, 0): 41, (1, 1): 72, (2, 0): 64, (2, 1): 68}
+ROUNDED_KIB = {(0, 0): 64, (0, 1): 68, (1, 0): 68, (1, 1): 64, (2, 0): 72, (2, 1): 68}
 
 
 def tile_list_paged_relu2_compact_kernel(
@@ -74,18 +74,18 @@ def tile_list_paged_relu2_compact_kernel(
         nc.sync.dma_start(gain_sb[:], gain.rearrange("(g p t) -> p g t", p=P, t=PACK))
         offs2_sb = keep.tile([P, S // LIST_ROWS], U16, name="offs2_sb")
         nc.sync.dma_start(offs2_sb[:], offs2)
-        load_w1(0, 0, 0)
         tab_scale_sb = keep.tile([P, T // 4], I32, name="tab_scale_sb", align_bytes=64)
         nc.vector.memset(tab_scale_sb[:], 0)
         tab_scale_hbm = tab_scales.bitcast(I32)
         for a in range(K_PASSES):
             nc.sync.dma_start(tab_scale_sb[4 * a : P : 8, :], tab_scale_hbm[a])
-        load_w1(0, 1, 8)
         tab_word_sb = []
         for a in range(K_PASSES):
             words = placed([P, T], I32, "tab_word%d" % a, 20 + 24 * a)
             nc.sync.dma_start(words[:], tab_words[a].rearrange("p t i -> p (t i)").bitcast(I32))
             tab_word_sb.append(words)
+        load_w1(0, 0, 0)
+        load_w1(0, 1, 8)
 
         gain_flat = gain_sb[:].rearrange("p g t -> p (g t)")
         width = GROUPS * PACK
@@ -114,7 +114,7 @@ def tile_list_paged_relu2_compact_kernel(
         nc.vector.tensor_copy(picked_scales[:], tab_scale_sb[:].bitcast(U8).indirect(offs_sb[:]))
 
         slots = []
-        for n in range(ROW_TILES - 1):
+        for n in range(ROW_TILES):
             rows_out = keep.tile([P, T2], F32, name="slots%d" % n)
             nc.vector.memset(rows_out[:], 0.0)
             slots.append(rows_out)
@@ -203,7 +203,10 @@ def tile_list_paged_relu2_compact_kernel(
                 h = keep.tile(shape, BF16, name="h" + name, align_bytes=64)
             else:
                 h = placed(shape, BF16, "h" + name, kib)
-            signed = h if signed_kib is None else placed(shape, BF16, "signed" + name, signed_kib)
+            if signed_kib is None:
+                signed = keep.tile(shape, BF16, name="signed" + name, align_bytes=64)
+            else:
+                signed = placed(shape, BF16, "signed" + name, signed_kib)
             if words_kib is None:
                 words = keep.tile([P, len(groups), CHUNK], U32, name="h_words" + name, align_bytes=64)
             else:
@@ -275,43 +278,40 @@ def tile_list_paged_relu2_compact_kernel(
 
         halves = [slice(0, P), slice(P, CHUNK)]
         up, down = (0, 1, 2), (2, 1, 0)
-        prepare_w1(0, 0, "scalar")
-        for half in range(2):
-            round_w1(0, 1, half, "scalar")
-        v_scales = placed([P, S], U8, "v_scales", 8)
+        v_scales = keep.tile([P, S], U8, name="v_scales", align_bytes=64)
         nc.vector.tensor_copy(v_scales[:].bitcast(I32), picked_scales[:].bitcast(I32))
         for a, i in [(a, i) for a in range(K_PASSES) for i in range(1, 4)]:
             src, dst = 4 * a + 8 * i, 4 * a + i
             nc.scalar.dma_start(v_scales[dst:P:32].bitcast(I32), picked_scales[src:P:32].bitcast(I32))
 
         gather_words(0, 0, 4)
+        load_w1(1, 0, 20)
+        load_w1(1, 1, 28)
+        gather_words(1, 0, 4)
+        load_w1(2, 0, 44)
+        load_w1(2, 1, 52)
+        prepare_w1(0, 0, "scalar")
+        round_w1(0, 1, 0, "vector")
+        round_w1(0, 1, 1, "scalar")
         for half in range(2):
             quantise_w1(0, 1, half)
-        load_w1(1, 0, 16)
-        slots.append(placed([P, T2], F32, "slots3", 24))
-        nc.vector.memset(slots[3][:], 0.0)
-        load_w1(1, 1, 32)
-        gather_words(1, 0, 2)
-        gather_words(1, 2, 2)
-        load_w1(2, 0, 45)
-        load_w1(2, 1, 53)
         prepare_w1(1, 0, "vector")
         prepare_w1(1, 1, "vector")
-        w2_word_sb = placed([P, GROUPS, 2 * N], U8, "w2_word_sb", 32)
+        w2_word_sb = placed([P, GROUPS, 2 * N], U8, "w2_word_sb", 28)
         nc.sync.dma_start(w2_word_sb[:].bitcast(I32), w2_words.bitcast(I32).rearrange("g p c -> p g c"))
-        wgo_sb = placed([P, S], F32, "wgo_sb", 35)
+        wgo_sb = placed([P, S], F32, "wgo_sb", 31)
         nc.sync.dma_start(wgo_sb[:], wgo)
-        b2_sb = placed([P, ROW_TILES], F32, "b2_sb", 39)
+        b2_sb = placed([P, ROW_TILES], F32, "b2_sb", 35)
         with nc.allow_non_contiguous_dma(reason="one bias value for each partition and row tile"):
             nc.sync.dma_start(b2_sb[:], b2.rearrange("(n p) -> p n", p=P))
-        w2_scale_sb = placed([P, GROUPS, N], U8, "w2_scale_sb", 72)
+        w2_scale_sb = placed([P, GROUPS, N], U8, "w2_scale_sb", 64)
         nc.vector.memset(w2_scale_sb[:].bitcast(I32), 0)
         w2_scale_hbm = w2_scales.bitcast(I32).rearrange("g q c -> q g c")
         for q in range(QUADRANTS):
             nc.sync.dma_start(w2_scale_sb[32 * q : 32 * q + 4].bitcast(I32), w2_scale_hbm[4 * q : 4 * q + 4])
-        batch(0, (0, 1), signed_kib=53)
+        batch(0, (0, 1), signed_kib=52)
         batch(0, (2,), kib=10, words_kib=4)
-        batch(1, (0, 1), signed_kib=57)
+        batch(1, (0,), signed_kib=56)
         rectify(0, 0, 2)
         square(0, 0)
         square(0, 1)
@@ -320,8 +320,7 @@ def tile_list_paged_relu2_compact_kernel(
 
         rectify(1, 0, 2)
         square(1, 0)
-        square(1, 1)
-        rectify(2, 0, 1)
+        rectify(2, 0, 1, kib=12)
         for part in halves:
             square(2, 0, part)
         apply_sign(0, 0)
@@ -336,20 +335,25 @@ def tile_list_paged_relu2_compact_kernel(
         add_bias(0, 1)
         apply_sign(0, 1)
         quantise_h(0, 1)
+        batch(1, (1,), kib=12)
+        square(1, 1)
+        apply_sign(1, 1)
+        quantise_h(1, 1)
         rectify(2, 1, 1)
-        rectify(0, 2, 1)
+        rectify(0, 2, 1, kib=20)
         batch(1, (2,), kib=4.5)
         square(2, 1)
         apply_sign(2, 1)
         quantise_h(2, 1)
         add_bias(0, 2)
-        rectify(1, 2, 1)
+        rectify(1, 2, 1, kib=24)
         batch(2, (0, 1))
         batch(2, (2,))
         square(0, 2)
         add_bias(0, 3)
-        rectify(2, 2, 1)
-        project(1, down, down)
+        rectify(2, 2, 1, kib=44)
+        project(1, up, (0, 1))
+        project(1, up, (2,))
         add_bias(1, 0)
         add_bias(1, 1)
         square(1, 2)
@@ -359,8 +363,8 @@ def tile_list_paged_relu2_compact_kernel(
         quantise_h(0, 2)
         quantise_h(2, 2)
         add_bias(1, 2)
-        rectify(0, 3, 1)
-        rectify(1, 3, 1)
+        rectify(0, 3, 1, kib=48)
+        rectify(1, 3, 1, kib=36)
         add_bias(1, 3)
         batch(3, (0, 1))
         batch(3, (2,), kib=0, signed_kib=2)
@@ -368,7 +372,7 @@ def tile_list_paged_relu2_compact_kernel(
         project(2, down, down)
         add_bias(2, 0)
         add_bias(2, 1)
-        rectify(2, 3, 1)
+        rectify(2, 3, 1, kib=40)
         square(1, 3)
         square(2, 3)
         apply_sign(0, 3)

@@ -74,16 +74,20 @@ def tile_list_paged_relu2_compact_kernel(
         nc.sync.dma_start(gain_sb[:], gain.rearrange("(g p t) -> p g t", p=P, t=PACK))
         offs2_sb = keep.tile([P, S // LIST_ROWS], U16, name="offs2_sb")
         nc.sync.dma_start(offs2_sb[:], offs2)
-        tab_scale_sb = keep.tile([P, T // 4], I32, name="tab_scale_sb", align_bytes=64)
+        tab_word_sb = []
+
+        def load_table(a):
+            words = placed([P, T], I32, "tab_word%d" % a, 20 + 24 * a)
+            nc.sync.dma_start(words[:], tab_words[a].rearrange("p t i -> p (t i)").bitcast(I32))
+            tab_word_sb.append(words)
+
+        load_table(0)
+        tab_scale_sb = placed([P, T // 4], I32, "tab_scale_sb", 76)
         nc.vector.memset(tab_scale_sb[:], 0)
         tab_scale_hbm = tab_scales.bitcast(I32)
         for a in range(K_PASSES):
             nc.sync.dma_start(tab_scale_sb[4 * a : P : 8, :], tab_scale_hbm[a])
-        tab_word_sb = []
-        for a in range(K_PASSES):
-            words = placed([P, T], I32, "tab_word%d" % a, 20 + 24 * a)
-            nc.sync.dma_start(words[:], tab_words[a].rearrange("p t i -> p (t i)").bitcast(I32))
-            tab_word_sb.append(words)
+        load_table(1)
         load_w1(0, 0, 0)
         load_w1(0, 1, 8)
 
@@ -122,7 +126,10 @@ def tile_list_paged_relu2_compact_kernel(
         v_words = {}
 
         def gather_words(a, first, count):
-            picked = keep.tile([P, CHUNK * count], U32, name="v_words%d%d" % (a, first), align_bytes=64)
+            if a == 0:
+                picked = placed([P, CHUNK * count], U32, "v_words0", 76)
+            else:
+                picked = keep.tile([P, CHUNK * count], U32, name="v_words1", align_bytes=64)
             entries = offs_sb[:, CHUNK // LIST_ROWS * first : CHUNK // LIST_ROWS * (first + count)]
             nc.vector.tensor_copy(picked[:], tab_word_sb[a][:].bitcast(U32).indirect(entries))
             for c in range(count):

from contextlib import ExitStack

import concourse.mybir as mybir

K, H, N, T, S, T2 = 1024, 1536, 512, 4096, 1024, 2048
FLOPS = 2 * K * H * S + 2 * H * N * S

F32 = mybir.dt.float32
BF16 = mybir.dt.bfloat16
I32 = mybir.dt.int32
U32 = mybir.dt.uint32
U16 = mybir.dt.uint16
U8 = mybir.dt.uint8
FP8X4 = mybir.dt.float8_e4m3fn_x4
FP4X4 = mybir.dt.float4_e2m1fn_x4
ALU = mybir.AluOpType
ACT = mybir.ActivationFunctionType

P = 128
PACK = 4
PASS = P * PACK
K_PASSES = K // PASS
GROUPS = H // PASS
ROW_TILES = N // P
CHUNK = 256
CHUNKS = S // CHUNK
LIST_ROWS = 16
BANK = 512
QUADRANTS = 4
TINY = 1e-30


VECTOR_TOKENS = 160
A_BANKS = {
    (0, 0): (0, 1, 2, 3),
    (1, 0): (4, 5, 6, 7),
    (2, 0): (0, 1),
    (2, 1): (2, 3),
    (0, 2): (0, 1),
    (1, 2): (4, 5),
    (2, 2): (6, 1),
    (0, 3): (4, 5),
    (1, 3): (6, 1),
    (2, 3): (0, 2),
}
Y_BANKS = [(4, 5, 6, 7), (0, 2, 3, 7), (4, 5, 3, 7), (6, 1, 0, 2)]
ROUNDED_KIB = {(0, 0): 64, (0, 1): 68, (1, 0): 68, (1, 1): 64, (2, 0): 72, (2, 1): 68}


def tile_list_paged_relu2_compact_kernel(
    tc, tab_words, tab_scales, offs, w1, gain, w2_words, w2_scales, b2, wgo, offs2, out
):
    nc = tc.nc
    with ExitStack() as ctx:
        keep = ctx.enter_context(tc.tile_pool(name="keep", bufs=1))
        reused = ctx.enter_context(tc.tile_pool(name="reused", bufs=1))

        def placed(shape, dtype, name, kib):
            return reused.tile(shape, dtype, name=name, offset=int(kib * 1024), align_bytes=64)

        psum = ctx.enter_context(tc.psum_pool(name="psum", bufs=1))

        w1_raw = {}

        def load_w1(g, a, kib):
            piece = placed([P, PACK, PASS], F32, "w1_raw%d%d" % (g, a), kib)
            rows = w1[PASS * a : PASS * (a + 1), PASS * g : PASS * (g + 1)]
            nc.sync.dma_start(piece[:], rows.rearrange("(p j) c -> p j c", j=PACK))
            w1_raw[g, a] = piece

        offs_sb = keep.tile([P, S // LIST_ROWS], U16, name="offs_sb")
        nc.sync.dma_start(offs_sb[:], offs)
        gain_sb = keep.tile([P, GROUPS, PACK], F32, name="gain_sb")
        nc.sync.dma_start(gain_sb[:], gain.rearrange("(g p t) -> p g t", p=P, t=PACK))
        offs2_sb = keep.tile([P, S // LIST_ROWS], U16, name="offs2_sb")
        nc.sync.dma_start(offs2_sb[:], offs2)
        tab_word_sb = []

        def load_table(a):
            words = placed([P, T], I32, "tab_word%d" % a, 20 + 24 * a)
            nc.sync.dma_start(words[:], tab_words[a].rearrange("p t i -> p (t i)").bitcast(I32))
            tab_word_sb.append(words)

        load_table(0)
        tab_scale_sb = placed([P, T // 4], I32, "tab_scale_sb", 76)
        nc.vector.memset(tab_scale_sb[:], 0)
        tab_scale_hbm = tab_scales.bitcast(I32)
        for a in range(K_PASSES):
            nc.sync.dma_start(tab_scale_sb[4 * a : P : 8, :], tab_scale_hbm[a])
        load_table(1)
        load_w1(0, 0, 0)
        load_w1(0, 1, 8)

        gain_flat = gain_sb[:].rearrange("p g t -> p (g t)")
        width = GROUPS * PACK
        size = keep.tile([P, width], F32, name="size")
        nc.vector.scalar_tensor_tensor(size[:], gain_flat, -1.0, gain_flat, ALU.mult, ALU.max)
        floored = keep.tile([P, width], F32, name="floored")
        nc.vector.tensor_scalar(floored[:], size[:], TINY, None, ALU.max)
        root0 = keep.tile([P, width], F32, name="root0")
        nc.scalar.activation(root0[:], floored[:], ACT.Sqrt)
        positive = keep.tile([P, width], F32, name="positive")
        nc.vector.tensor_scalar(positive[:], gain_flat, 0.0, None, ALU.is_gt)
        negative = keep.tile([P, width], F32, name="negative")
        nc.vector.tensor_scalar(negative[:], gain_flat, 0.0, None, ALU.is_lt)
        sign = keep.tile([P, GROUPS, PACK], BF16, name="sign")
        nc.vector.tensor_tensor(sign[:].rearrange("p g t -> p (g t)"), positive[:], negative[:], ALU.subtract)
        inverse = keep.tile([P, width], F32, name="inverse")
        nc.vector.reciprocal(inverse[:], root0[:])
        quotient = keep.tile([P, width], F32, name="quotient")
        nc.vector.tensor_tensor(quotient[:], floored[:], inverse[:], ALU.mult)
        twice_root = keep.tile([P, width], F32, name="twice_root")
        nc.vector.tensor_tensor(twice_root[:], quotient[:], root0[:], ALU.add)
        root = keep.tile([P, width], F32, name="root")
        nc.vector.tensor_scalar(root[:], twice_root[:], 0.5, None, ALU.mult)

        picked_scales = keep.tile([P, S], U8, name="picked_scales", align_bytes=64)
        nc.vector.tensor_copy(picked_scales[:], tab_scale_sb[:].bitcast(U8).indirect(offs_sb[:]))

        slots = []
        for n in range(ROW_TILES):
            rows_out = keep.tile([P, T2], F32, name="slots%d" % n)
            nc.vector.memset(rows_out[:], 0.0)
            slots.append(rows_out)

        v_words = {}

        def gather_words(a, first, count):
            if a == 0:
                picked = placed([P, CHUNK * count], U32, "v_words0", 76)
            else:
                picked = keep.tile([P, CHUNK * count], U32, name="v_words1", align_bytes=64)
            entries = offs_sb[:, CHUNK // LIST_ROWS * first : CHUNK // LIST_ROWS * (first + count)]
            nc.vector.tensor_copy(picked[:], tab_word_sb[a][:].bitcast(U32).indirect(entries))
            for c in range(count):
                v_words[a, first + c] = (picked, c)

        w1_rounded, w1_words, w1_scales = {}, {}, {}

        def round_w1(g, a, half, engine):
            if half == 0:
                w1_rounded[g, a] = placed([P, PACK * PASS], BF16, "r%d%d" % (g, a), ROUNDED_KIB[g, a])
            dst = w1_rounded[g, a][:].rearrange("p (t m j) -> p m j t", t=PACK, j=PACK)
            src = w1_raw[g, a][:].rearrange("p j (m t) -> p m j t", t=PACK)
            pair = slice(2 * half, 2 * half + 2)
            if engine == "scalar":
                nc.scalar.copy(dst[:, :, :, pair], src[:, :, :, pair])
            else:
                nc.vector.tensor_copy(dst[:, :, :, pair], src[:, :, :, pair])

        def quantise_w1(g, a, half):
            if half == 0:
                w1_words[g, a] = keep.tile([P, PASS], U32, name="w1_words%d%d" % (g, a), align_bytes=64)
                w1_scales[g, a] = keep.tile([P, PASS], U8, name="w1_scales%d%d" % (g, a), align_bytes=64)
            cols = slice(PASS // 2 * half, PASS // 2 * (half + 1))
            nc.vector.quantize_mx(
                out=w1_words[g, a][:, cols].bitcast(FP8X4),
                scales=w1_scales[g, a][:, cols],
                in_=w1_rounded[g, a][:, PACK * cols.start : PACK * cols.stop],
            )

        def prepare_w1(g, a, engine):
            for half in range(2):
                round_w1(g, a, half, engine)
            for half in range(2):
                quantise_w1(g, a, half)

        h_tiles, batches, h_words, h_scales, rectified, y_acc, y_parts = {}, {}, {}, {}, {}, {}, {}
        y_sb = [keep.tile([P, S], F32, name="y%d" % n) for n in range(ROW_TILES)]

        def rectify(g, first, count, vector_banks=(), kib=None):
            width = CHUNK * count
            tokens = slice(CHUNK * first, CHUNK * first + width)
            per_bank = BANK // width
            if kib is None:
                values = keep.tile([P, PACK, width], F32, name="values%d%d" % (first, g), align_bytes=64)
            else:
                values = placed([P, PACK, width], F32, "values%d%d" % (first, g), kib)
            for bank in range(PACK // per_bank):
                where = A_BANKS[g, first][bank] * BANK * 4
                acc = psum.tile([P, per_bank, width], F32, name="a%d%d%d" % (g, first, bank), offset=where)
                for a in range(K_PASSES):
                    picked, c = v_words[a, first]
                    for u in range(per_bank):
                        t = per_bank * bank + u
                        cols = slice(P * t, P * (t + 1))
                        nc.tensor.matmul_mx(
                            out=acc[:, u, :],
                            lhsT=w1_words[g, a][:, cols].bitcast(FP8X4),
                            lhsT_scale=w1_scales[g, a][:, cols],
                            rhs=picked[:, CHUNK * c : CHUNK * c + width].bitcast(FP8X4),
                            rhs_scale=v_scales[4 * a :, tokens],
                            start=(a == 0 and u == 0),
                            stop=(a == K_PASSES - 1 and u == per_bank - 1),
                        )
                for u in range(per_bank):
                    t = per_bank * bank + u
                    factor = root[:, PACK * g + t : PACK * g + t + 1]
                    if bank in vector_banks:
                        nc.vector.tensor_scalar(values[:, t, :], acc[:, u, :], 0.0, factor, ALU.max, ALU.mult)
                    else:
                        nc.scalar.activation(values[:, t, :], acc[:, u, :], ACT.Relu, scale=factor)
            for c in range(count):
                rectified[first + c, g] = values[:, :, CHUNK * c : CHUNK * (c + 1)]

        def batch(c, groups, kib=None, signed_kib=None, words_kib=None):
            name = "%d%d" % (c, groups[0])
            shape = [P, len(groups), CHUNK * PACK]
            if kib is None:
                h = keep.tile(shape, BF16, name="h" + name, align_bytes=64)
            else:
                h = placed(shape, BF16, "h" + name, kib)
            if signed_kib is None:
                signed = keep.tile(shape, BF16, name="signed" + name, align_bytes=64)
            else:
                signed = placed(shape, BF16, "signed" + name, signed_kib)
            if words_kib is None:
                words = keep.tile([P, len(groups), CHUNK], U32, name="h_words" + name, align_bytes=64)
            else:
                words = placed([P, len(groups), CHUNK], U32, "h_words" + name, words_kib)
            scales = keep.tile([P, len(groups), CHUNK], U8, name="h_scales" + name, align_bytes=64)
            batches[c, groups[0]] = (groups, h, signed, words, scales)
            for i, g in enumerate(groups):
                h_tiles[c, g], h_words[c, g], h_scales[c, g] = h[:, i, :], words[:, i, :], scales[:, i, :]

        def square(g, c, part=slice(0, CHUNK), engine="scalar"):
            runs = "p (c i) t -> p c t i"
            dst = h_tiles[c, g].rearrange("p (c t) -> p c t", t=PACK)[:, part]
            src = rectified[c, g][:, :, part].rearrange("p t c -> p c t")
            dst, src = dst.rearrange(runs, i=PACK), src.rearrange(runs, i=PACK)
            if engine == "scalar":
                nc.scalar.activation(dst, src, ACT.Square)
            else:
                nc.vector.tensor_tensor(dst, src, src, ALU.mult)

        def apply_sign(g, c, part=slice(0, CHUNK)):
            groups, h, signed, words, scales = batches[c, g]
            src = h[:].rearrange("p g (c t) -> p g c t", t=PACK)[:, :, part]
            dst = signed[:].rearrange("p g (c t) -> p g c t", t=PACK)[:, :, part]
            signs = sign[:, g : g + len(groups), :].unsqueeze(2)
            signs = signs.to_broadcast([P, len(groups), part.stop - part.start, PACK])
            nc.vector.tensor_tensor(dst, src, signs, ALU.mult)

        def quantise_h(g, c, part=slice(0, CHUNK)):
            groups, h, signed, words, scales = batches[c, g]
            cols = slice(part.start, part.stop + CHUNK * (len(groups) - 1))
            nc.vector.quantize_mx(
                out=words[:].rearrange("p g c -> p (g c)")[:, cols].bitcast(FP8X4),
                scales=scales[:].rearrange("p g c -> p (g c)")[:, cols],
                in_=signed[:].rearrange("p g c -> p (g c)")[:, PACK * cols.start : PACK * cols.stop],
            )

        def project(c, order, groups):
            for n in range(ROW_TILES):
                if groups[0] == order[0]:
                    y_acc[c, n] = psum.tile([P, CHUNK], F32, name="y%d%d" % (c, n), offset=Y_BANKS[c][n] * BANK * 4)
                passes = [(g, first) for g in order for first in range(0, CHUNK, P)]
                for g, first in passes:
                    if g not in groups:
                        continue
                    part = slice(first, first + P)
                    nc.tensor.matmul_mx(
                        out=y_acc[c, n][:, part],
                        lhsT=w2_word_sb[:, g, 2 * P * n : 2 * P * (n + 1)].bitcast(FP4X4),
                        lhsT_scale=w2_scale_sb[:, g, P * n : P * (n + 1)],
                        rhs=h_words[c, g][:, part].bitcast(FP8X4),
                        rhs_scale=h_scales[c, g][:, part],
                        start=((g, first) == passes[0]),
                        stop=((g, first) == passes[-1]),
                    )

        def add_bias(c, n, kib=None):
            dst = y_sb[n][:, CHUNK * c : CHUNK * (c + 1)]
            if kib is not None:
                dst = placed([P, CHUNK], F32, "y_late", kib)[:]
                y_parts[n, c] = dst
            nc.scalar.activation(dst, y_acc[c, n][:], ACT.Identity, bias=b2_sb[:, n : n + 1])

        def scatter(n, first, last):
            places = offs2_sb[:, CHUNK // LIST_ROWS * first : CHUNK // LIST_ROWS * last]
            tokens = slice(CHUNK * first, CHUNK * last)
            nc.vector.tensor_tensor(slots[n][:].indirect(places), y_parts.get((n, first), y_sb[n][:, tokens]), wgo_sb[:, tokens], ALU.mult)
            if last == CHUNKS:
                nc.sync.dma_start(out[P * n : P * (n + 1), :], slots[n][:])

        halves = [slice(0, P), slice(P, CHUNK)]
        up, down = (0, 1, 2), (2, 1, 0)
        v_scales = keep.tile([P, S], U8, name="v_scales", align_bytes=64)
        nc.vector.tensor_copy(v_scales[:].bitcast(I32), picked_scales[:].bitcast(I32))
        for a, i in [(a, i) for a in range(K_PASSES) for i in range(1, 4)]:
            src, dst = 4 * a + 8 * i, 4 * a + i
            nc.scalar.dma_start(v_scales[dst:P:32].bitcast(I32), picked_scales[src:P:32].bitcast(I32))

        gather_words(0, 0, 4)
        load_w1(1, 0, 20)
        load_w1(1, 1, 28)
        gather_words(1, 0, 4)
        load_w1(2, 0, 44)
        load_w1(2, 1, 52)
        prepare_w1(0, 0, "scalar")
        round_w1(0, 1, 0, "vector")
        round_w1(0, 1, 1, "scalar")
        for half in range(2):
            quantise_w1(0, 1, half)
        prepare_w1(1, 0, "vector")
        prepare_w1(1, 1, "vector")
        w2_word_sb = placed([P, GROUPS, 2 * N], U8, "w2_word_sb", 28)
        nc.sync.dma_start(w2_word_sb[:].bitcast(I32), w2_words.bitcast(I32).rearrange("g p c -> p g c"))
        wgo_sb = placed([P, S], F32, "wgo_sb", 31)
        nc.sync.dma_start(wgo_sb[:], wgo)
        b2_sb = placed([P, ROW_TILES], F32, "b2_sb", 35)
        with nc.allow_non_contiguous_dma(reason="one bias value for each partition and row tile"):
            nc.sync.dma_start(b2_sb[:], b2.rearrange("(n p) -> p n", p=P))
        w2_scale_sb = placed([P, GROUPS, N], U8, "w2_scale_sb", 64)
        nc.vector.memset(w2_scale_sb[:].bitcast(I32), 0)
        w2_scale_hbm = w2_scales.bitcast(I32).rearrange("g q c -> q g c")
        for q in range(QUADRANTS):
            nc.sync.dma_start(w2_scale_sb[32 * q : 32 * q + 4].bitcast(I32), w2_scale_hbm[4 * q : 4 * q + 4])
        batch(0, (0, 1), signed_kib=52)
        batch(0, (2,), kib=10, words_kib=4)
        batch(1, (0,), signed_kib=56)
        rectify(0, 0, 2)
        square(0, 0)
        square(0, 1)
        prepare_w1(2, 0, "vector")
        prepare_w1(2, 1, "vector")

        rectify(1, 0, 2)
        square(1, 0)
        rectify(2, 0, 1, kib=12)
        for part in halves:
            square(2, 0, part)
        apply_sign(0, 0)
        quantise_h(0, 0)
        project(0, up, (0, 1))
        for part in halves:
            apply_sign(2, 0, part)
        for part in halves:
            quantise_h(2, 0, part)
        project(0, up, (2,))
        add_bias(0, 0)
        add_bias(0, 1)
        apply_sign(0, 1)
        quantise_h(0, 1)
        batch(1, (1,), kib=12)
        square(1, 1)
        apply_sign(1, 1)
        quantise_h(1, 1)
        rectify(2, 1, 1)
        rectify(0, 2, 1, kib=20)
        batch(1, (2,), kib=4.5)
        square(2, 1)
        apply_sign(2, 1)
        quantise_h(2, 1)
        add_bias(0, 2)
        rectify(1, 2, 1, kib=24)
        batch(2, (0, 1))
        batch(2, (2,))
        square(0, 2)
        add_bias(0, 3)
        rectify(2, 2, 1, kib=44)
        project(1, up, (0, 1))
        project(1, up, (2,))
        add_bias(1, 0)
        add_bias(1, 1)
        square(1, 2)
        square(2, 2)
        apply_sign(0, 2)
        apply_sign(2, 2)
        quantise_h(0, 2)
        quantise_h(2, 2)
        add_bias(1, 2)
        rectify(0, 3, 1, kib=48)
        rectify(1, 3, 1, kib=36)
        add_bias(1, 3)
        batch(3, (0, 1))
        batch(3, (2,), kib=0, signed_kib=2)
        square(0, 3)
        project(2, down, down)
        add_bias(2, 0)
        add_bias(2, 1)
        rectify(2, 3, 1, kib=40)
        square(1, 3)
        square(2, 3)
        apply_sign(0, 3)
        apply_sign(2, 3)
        quantise_h(0, 3)
        quantise_h(2, 3)
        add_bias(2, 3)
        add_bias(2, 2, kib=0)
        project(3, up, up)
        for n in range(ROW_TILES):
            add_bias(3, n)
        for c in range(2):
            for n in range(ROW_TILES):
                scatter(n, c, c + 1)
        for c in range(2, CHUNKS):
            for n in range(ROW_TILES - 1):
                scatter(n, c, c + 1)
        scatter(3, 2, 4)
